import numpy as np, ml_dtypes
CORES = [3,7,11,15,131,135,139,143]
N = 8
import mx_ref
BF = ml_dtypes.bfloat16
def gcols(t, e):
    v = np.concatenate([t.reshape(8, 16, -1, 4), np.zeros((8, 16, 1, 4), BF)], axis=2)
    return np.ascontiguousarray(np.stack([v[g][:, e[g]] for g in range(8)])).reshape(128, -1)
def tile(rs):
    return np.stack(rs, axis=2).reshape(128, -1).astype(BF)
def cut(t, i, w=512):
    return t[:, w * i:w * i + w]
def pick(q, e):
    c = np.concatenate([q[0].reshape(128, -1, 4), np.zeros((128, 1, 4), np.uint8)], axis=1); s = np.concatenate([q[1], np.ones((16, 1), np.uint8)], axis=1)
    return (np.ascontiguousarray(c[:, e].reshape(128, -1)), np.ascontiguousarray(s[:, e]))
def join(*qs):
    return (np.concatenate([q[0] for q in qs], axis=1), np.concatenate([q[1] for q in qs], axis=1))
def put(q, e, v):
    c, s = q[0].reshape(128, -1, 4).copy(), q[1].copy(); c[:, e] = v[0].reshape(128, -1, 4); s[:, e] = v[1]
    return (c.reshape(128, -1), s)
def pk(c, s):
    return (np.ascontiguousarray(c), mx_ref.live(s))
def emit(q):
    return q[0], q[1]
def packed(v, rng):
    q = [mx_ref.quantize(np.ascontiguousarray(v[r])) for r in range(N)]
    return np.stack([a for a, b in q]), np.stack([mx_ref.plane(b, rng) for a, b in q])
def values_of_codes():
    e, c = np.zeros((128, 128, 4), np.float32), np.zeros((128, 2, 4), np.uint8)
    e[np.arange(128), np.arange(128), 0] = 1
    c[:127, :, 0] = np.arange(256).reshape(2, 128).T[:127]
    return mx_ref.matmul(mx_ref.quantize(e.reshape(128, 512).astype(BF)), (c.reshape(128, 8), np.full((16, 2), 127, np.uint8))).T.reshape(-1).astype(np.float64)
CODE_VALUE, SCALE_VALUE = values_of_codes(), 2.0 ** (np.arange(256) - 127.0)
def decode(q):
    return (CODE_VALUE[q[0]].reshape(16, 8, -1, 4) * SCALE_VALUE[q[1]][:, None, :, None] + 0.0).reshape(128, -1).astype(np.float32)
def f(rng, *shape):
    return mx_ref.flush((rng.standard_normal(shape, dtype=np.float32) * np.exp2(rng.integers(-2, 3, shape[:-1] + (1,)))).astype(BF))
def wide(rng, *shape, cols=0):
    v = rng.standard_normal(shape, dtype=np.float32) * np.exp2(rng.integers(-12, 13, shape)).astype(np.float32)
    if cols: v *= np.repeat(np.exp2(rng.integers(-cols, cols + 1, shape[:-2] + (1, shape[-1] // 4))) * (rng.random(shape[:-2] + (1, shape[-1] // 4)) > 0.0625), 4, axis=-1).astype(np.float32)
    return mx_ref.flush(v.astype(BF))
C, H, A, L, R = 320, 4, 10, 96, 3
def buckets(p):
    bit = p.reshape(8, 16, C)[:, :H] + np.float32(0.0) >= 0
    leaf = np.zeros((8, C), np.int64)
    for i in range(H): leaf = 2 * leaf + bit[:, i]
    at, slot = np.full((8, C), -1), np.zeros((8, C), np.int64)
    before = np.arange(C)[:, None] > np.arange(C)
    for v in range(H, -1, -1):
        way = (1 << v) - 1 + (leaf >> (H - v))
        free = at < 0
        n = np.sum((way[:, :, None] == way[:, None, :]) & free[:, None, :] & before, axis=2)
        new = free & (n < A)
        at[new] = way[new]
        slot[new] = n[new]
    return at, slot
def mates(at, slot):
    own = np.tile(np.arange(C), (8, 1))
    held = np.full((8, 2 << H, A), -1)
    g, j = np.nonzero(at >= 0)
    held[g, at[g, j], slot[g, j]] = j
    e = held[np.arange(8)[:, None], (at - 1) // 2, slot]
    return np.where((at > 0) & (e >= 0), e, own)
def big(v):
    v = v.astype(np.float32)
    v[np.abs(v) < np.float32(2.0 ** -16)] = 0
    return v.astype(BF)
def numbers_of(rng):
    return {"x": big(f(rng, N, 128, 4 * C)), "u": np.array(f(rng, N, 128, 512)), "v": np.array(f(rng, N, 128, 512))}
def weights(rng, w):
    c, p = packed(w, rng)
    return {"wc": c, "ws": p}
def still(rng, k, more=0):
    w = np.zeros((N, 128, 4, 128, 4), np.float32)
    i = np.arange(128)
    for b in range(4): w[:, i, b, i, b] = k
    e = i[15::16]
    w[:, e, 0, e, 1] = more
    return weights(rng, w.reshape(N, 128, 2048).astype(BF))
MARKS = np.array([[[0, 1], [1, 2], [0, 1], [1, 2], [1, 0], [1, 1], [2, 1], [0, 0]],
                  [[0, 1], [1, 2], [1, 1.125], [1.25, 1.375], [1, 0], [1, 1], [1.125, 1], [0, 0]]])
EDGES = [(10, 14), (10, 15), (10, 13)]
def marked(rng, d, leaf, size, k):
    x = d["x"].reshape(N, 8, 16, C, 4)
    u = d["u"].reshape(N, 128, 128, 4)
    x[:, :, :8] = 0
    fine = (size < 1).astype(int)[:, None, None]
    for i in range(H):
        bit = leaf >> (H - 1 - i) & 1
        x[:, :, i, :, :2] = (MARKS[fine, 4 * bit + rng.integers(0, 4, bit.shape)] * size[:, None, None, None]).astype(BF)
        for c in range(i, 128, 16):
            u[:, :, c] = 0
            u[:, c, c, 0] = k.astype(BF)
            u[:, c, c, 1] = (-k).astype(BF)
    return {"x": x.reshape(N, 128, 4 * C), "u": u.reshape(N, 128, 512), "v": d["v"]}
def setup_inputs(rng):
    return {**numbers_of(rng), **weights(rng, big(f(rng, N, 128, 2048)))}
def setup_inputs_leaves(rng):
    d = numbers_of(rng)
    o = rng.permutation(N)
    leaf = rng.integers(0, 1 << H, (N, 8, C))
    s = np.repeat(np.arange(8), [A, A, A + A // 2, 2 * A - A // 2, A + 1, 0, 0, A - 1])
    for r in range(N):
        for g in range(8):
            m = int(rng.integers(1 << H))
            if o[r] == 0: leaf[r, g] = m
            if o[r] == 1: leaf[r, g] = rng.permutation(np.concatenate([s, rng.integers(8, 1 << H, C - len(s))])) ^ m
            if o[r] == 3 and g % 4 == 0: leaf[r, g] = rng.permutation(np.arange(C) % (1 << H))
            if o[r] == 3 and g % 4 > 0:
                n, p = EDGES[g % 4 - 1]
                leaf[r, g] = rng.permutation(np.concatenate([n - 1 - np.arange(C - p) % n, np.full(p, n)])) ^ m
    d = marked(rng, d, leaf, np.ones(N), np.ones(N, np.float32))
    d["x"][o == 2] = 0
    return {**d, **still(rng, 64)}
def setup_inputs_near(rng):
    o = rng.permutation(N) % 4
    size = 2.0 ** np.array([-30.0, -30.0, 0.0, 10.0])[o]
    k = np.where(o < 2, 2.0 ** -30, 1.0).astype(np.float32)
    leaf = rng.integers(0, 1 << H, (N, 8, C)) & rng.integers(0, 1 << H, (N, 8, 1))
    return {**marked(rng, numbers_of(rng), leaf, size, k), **still(rng, 64)}
def setup_inputs_again(rng):
    d = numbers_of(rng)
    u = d["u"].reshape(N, 128, 128, 4)
    for g in range(0, 128, 16):
        for c in range(g, g + H):
            u[:, :, c] = 0
            u[:, c, c, 0] = 1
            u[:, c + 8, c, 0] = -1
    s = (N, 8, 16, C, 4)
    x = rng.integers(8, 16, s) * np.exp2(rng.integers(-21, -12, s))
    x[:, :, 8:8 + H, :, 0] = x[:, :, :H, :, 0] * rng.integers(1, 3, (N, 8, H, C))
    x[:, :, 7, :, 0] = 1.9921875
    x[:, :, 15, :, 0] = 1.875
    x[:, :, 15, :, 1] = 0.75
    return {"x": x.astype(np.float32).astype(BF).reshape(N, 128, 4 * C), "u": u.reshape(N, 128, 512), "v": d["v"], **still(rng, 64, 8)}
def setup_inputs_huge(rng):
    d = numbers_of(rng)
    o = rng.permutation(N)
    c = np.ones((N, C))
    s = rng.choice([-1.0, 1.0], (N, 128))
    for r in range(N):
        if o[r] == 0: s[r] = -1
        if o[r] == 1: s[r] = 1
        if o[r] > 2: c[r] = rng.permutation(C) % 2 * 2.0 - 1.0
    x = 2.0 ** 28 * (1.5 + 0.5 * rng.random((N, 128, C, 4))) * c[:, None, :, None]
    u = 2.0 ** 30 * (0.75 + 0.25 * rng.random((N, 128, 128, 4))) * s[:, None, :, None]
    return {"x": x.astype(np.float32).astype(BF).reshape(N, 128, 4 * C), "u": u.astype(np.float32).astype(BF).reshape(N, 128, 512), "v": d["v"], **still(rng, 32)}
def setup_inputs_spread(rng):
    d = setup_inputs(rng)
    d["x"] = big(wide(rng, N, 128, 4 * C, cols=6))
    return d
def check_inputs(d):
    b = []
    for k in ("x", "u", "v"):
        a = np.abs(d[k].astype(np.float32))
        if not (np.isfinite(a).all() and ((a == 0) | (a >= 2.0 ** -30) & (a <= 2.0 ** 30)).all()): b.append("a value of " + k)
    return b
def reference(x, u, v, wc, ws):
    qu = [mx_ref.quantize(u[r]) for r in range(N)]
    lay = [pk(wc[r], ws[r]) for r in range(N)]
    now = [x[r] for r in range(N)]
    for t in range(R):
        held, made, gone, sent = [], [], [], []
        for r in range(N):
            at, slot = buckets(mx_ref.matmul(qu[r], mx_ref.quantize(now[r])))
            met = gcols(now[r], mates(at, slot))
            q = mx_ref.quantize((now[r].astype(np.float32) + met.astype(np.float32)).astype(BF))
            h = tile([mx_ref.matmul(pick(lay[r], np.arange(128 * b, 128 * b + 128)), q) * np.float32(0.015625) for b in range(4)])
            e = np.argsort(at, axis=1, kind="stable")[:, :L]
            held.append(at)
            made.append(h)
            gone.append(e)
            sent.append(mx_ref.quantize(gcols(h, e)))
        came = decode(join(*sent)).astype(BF)
        for r in range(N):
            e = np.tile(np.arange(C), (8, 1))
            np.put_along_axis(e, gone[r], np.tile(C + np.arange(L), (8, 1)), axis=1)
            now[r] = gcols(np.concatenate([made[r], cut(came, (r - 1) % N, 4 * L)], axis=1), e)
    y, ob = np.zeros((N, 128, C), np.float32), np.zeros((N, 8, C), np.float32)
    oc, osc = np.zeros((N, 128, 4 * C), np.uint8), np.zeros((N, 16, C), np.uint8)
    for r in range(N):
        q = mx_ref.quantize(now[r])
        y[r] = mx_ref.matmul(mx_ref.quantize(v[r]), q)
        ob[r] = held[r]
        oc[r], osc[r] = emit(q)
    return {"y": y, "ob": ob, "oc": oc, "osc": osc}

@@ -1,0 +1,474 @@
+import numpy as np
+from concourse.mybir import dt, AluOpType, ActivationFunctionType
+
+A = AluOpType
+F = ActivationFunctionType
+C, L, R = 320, 96, 3
+TD = "float16"
+U = 2.0 ** -11
+B0 = 288
+OFF = {v: B0 + 32 * (1 << v) - 11 for v in range(5)}
+EMPTY = 2048.0
+MAGIC = 12582912.0
+CUT = 192
+E0 = 36
+Q4, U8, BF, F32, I32, U16 = "float8_e4m3fn_x4", "uint8", "bfloat16", "float32", "int32", "uint16"
+
+SCRATCH = {"ps": ("psum", [128, 4096], F32)}
+for _d, _list in (
+        (BF, "xx 3840 ut 512 vt 512 st 512 oh 1344 wf 512 wi 512 eb 516 zer 512 ones 128 unit 128 bd 128 wr 32 zt 1280 yd 1664 bt 512"),
+        (Q4, "qw 512 qu 128 qv 128 qx 320 qz 320 qs 128 qo 336 qf 128 qi 128 qe 512 qb0 128 qb1 128 qb2 128 qa0 224 qa1 224 qa2 224"),
+        (U8, "sw 512 su 128 sv 128 sx 320 sz 320 ss 128 so 336 sf 128 si 128 se 512 sb0 128 sb1 128 sb2 128 sa0 224 sa1 224 sa2 224"),
+        (F32, "cl 24 c4 24 mc0 336 mc 336 xm4 80 df 80 n16 21 n1 21 tl 64 rst 168 jv 320 s4 80 mm 320 x16 320 dw 320 sk0 96 sk 96 "
+              "d5 96 six 16 tb0 800 tb 800 obf 320 fs 84 nt0 63 nt 84 cnt 336 hh 800 gap 16 dd 16 fl 96 fd 96 fm 96 ge 96 es 96 "
+              "inv 320 ivs 320 yo 320"),
+        (TD, "rs2 336 rs3 336 dm 320 k4 336 k3 336 k2 168 k1 84 t4 336 t3 336 t2 168 t1 84 r4 336 r3 168 r2 84 r1 42 qq 2376 "
+             "vd 147 fin 147 gg 320 gs 320"),
+        (I32, "ci 8 tli 24 pos 20 pa 20 pc 20"),
+        (U16, "loh 22 ltr 22 lt4 22 lrep 6 lpos 20 lpp 20 lm 80 lfix 6 le 6 lsrc 20")):
+    _w = _list.split()
+    for _k in range(0, len(_w), 2):
+        SCRATCH[_w[_k]] = ("sbuf", [128, int(_w[_k + 1])], _d)
+NS = 100
+SEMAPHORES = ["s%d" % i for i in range(NS)] + ["arr0", "arr1", "arr2", "sent", "stored"]
+
+
+def emit(ops, queues, T):
+    known = {q: set() for q in queues}
+    groups = {}
+    for i, o in enumerate(ops):
+        groups.setdefault(o["grp"] or i, []).append(i)
+
+    def meet(xs, ys, only=None):
+        return any(n == n2 and only in (None, n) and (m & m2).any() for (n, m) in xs for (n2, m2) in ys)
+
+    seen, waits, needed = [], [], set()
+    for i, o in enumerate(ops):
+        mine = []
+        for k in range(i - 1, -1, -1):
+            e = ops[k]
+            if k in known[o["q"]] or e["kind"] in ("remote", "store"):
+                continue
+            if meet(o["w"], e["w"] + e["r"]) or meet(o["r"], e["w"]) or (e["q"] != o["q"] and meet(o["r"], e["r"], "ps")):
+                key = e["grp"] or k
+                assert groups[key][-1] < i
+                mine.append(key)
+                needed.add(key)
+                for j in groups[key]:
+                    known[o["q"]].add(j)
+                    known[o["q"]] |= seen[j]
+        waits.append(mine)
+        seen.append(set(known[o["q"]]))
+    last = []
+    tag = {}
+    for i, o in enumerate(ops):
+        key = o["grp"] or i
+        if key not in needed or key in tag:
+            continue
+        step = 16 if o["kind"] == "dma" else 1
+        cls = "dma" if o["kind"] == "dma" else "c"
+        pick = None
+        for s, (c, ks, n) in enumerate(last):
+            if c == cls and all(k in seen[j] for k in ks for j in groups[key]):
+                pick = s
+                break
+        if pick is None:
+            last.append([cls, [], 0])
+            pick = len(last) - 1
+        last[pick][1] = groups[key]
+        last[pick][2] += step * len(groups[key])
+        tag[key] = (pick, last[pick][2], step)
+    stores = 0
+    for i, o in enumerate(ops):
+        q = queues[o["q"]]
+        key = o["grp"] or i
+        for k in waits[i]:
+            q.wait_ge(T.sem["s%d" % tag[k][0]], tag[k][1])
+        for (s, n) in o["pre"]:
+            q.wait_ge(s, n)
+        ins = o["f"]()
+        if o["kind"] == "store":
+            ins.then_inc(T.sem.stored, 16)
+            stores += 16
+        elif key in tag:
+            ins.then_inc(T.sem["s%d" % tag[key][0]], tag[key][2])
+    queues["y"].wait_ge(T.sem.stored, stores)
+
+
+def engine_mask(topo, src, dst):
+    e = topo.engines(src, dst)
+    e = e[::len(e) // 8]
+    m = 0
+    for k in e:
+        m |= 1 << k
+    return m, len(e)
+
+
+def rank_program(g, core, T, topo):
+    rank = T.rank_of(core)
+    if rank is None:
+        return
+    n_ranks = len(T.cores)
+    nxt, prv = T.cores[(rank + 1) % n_ranks], T.cores[(rank - 1) % n_ranks]
+    rid, pid = topo.addr(nxt, core)
+    mask, n_out = engine_mask(topo, core, nxt)
+    n_in = engine_mask(topo, prv, core)[1]
+    queues = {"v": g.vector, "s": g.scalar, "t": g.tensor, "g": g, "y": g.sync}
+    ops = []
+
+    def V(name, a=0, b=None, step=1):
+        w = SCRATCH[name][1][1]
+        b = w if b is None else b
+        m = np.zeros(w, bool)
+        if name == "ps":
+            m[a // 512 * 512:(b + 511) // 512 * 512] = True
+        else:
+            m[a:b:step] = True
+        ap = T[name][:, a:b] if step == 1 else T[name][:, a:b:step]
+        return (ap, [(name, m)])
+
+    def I(win, off):
+        return (win[0].indirect(off[0]), win[1] + off[1])
+
+    def op(q, f, w, r, kind="c", pre=(), grp=None):
+        ww, rr = [], []
+        for x in w:
+            ww += x[1]
+        for x in r:
+            if isinstance(x, tuple):
+                rr += x[1]
+        ops.append({"q": q, "f": f, "w": ww, "r": rr, "kind": kind, "pre": list(pre), "grp": grp})
+
+    def a_(x):
+        return x[0] if isinstance(x, tuple) else x
+
+    def ts(out, x, s1, o0, s2=None, o1=None, grp=None):
+        if o1 is None:
+            op("v", lambda: g.vector.tensor_scalar(out[0], x[0], a_(s1), None, o0), [out], [x, s1], grp=grp)
+        else:
+            op("v", lambda: g.vector.tensor_scalar(out[0], x[0], a_(s1), a_(s2), o0, o1), [out], [x, s1, s2], grp=grp)
+
+    def tt(out, x, y, o, grp=None):
+        op("v", lambda: g.vector.tensor_tensor(out[0], x[0], y[0], o), [out], [x, y], grp=grp)
+
+    def cp(out, x, grp=None):
+        op("v", lambda: g.vector.tensor_copy(out[0], x[0]), [out], [x], grp=grp)
+
+    def scatter(win, off, x):
+        op("v", lambda: g.vector.tensor_copy(win[0].indirect(off[0]), x[0]), [win], [off, x])
+
+    def scan(out, d0, d1, o0, o1, grp=None):
+        op("v", lambda: g.vector.tensor_tensor_scan(out[0], d0[0], d1[0], 0.0, o0, o1), [out], [d0, d1], grp=grp)
+
+    def fill(out, c, grp=None):
+        op("v", lambda: g.vector.memset(out[0], c), [out], [], grp=grp)
+
+    def quant(name, a, b, x):
+        q, s = V("q" + name, a, b), V("s" + name, a, b)
+        op("v", lambda: g.vector.quantize_mx(q[0], s[0], x[0]), [q, s], [x])
+
+    def act(out, x, scale=1.0, bias=0.0, f=F.Identity, grp=None):
+        op("s", lambda: g.scalar.activation(out[0], x[0], f, bias=a_(bias), scale=a_(scale)), [out], [x, scale, bias], grp=grp)
+
+    def acp(out, x, scale=1.0, grp=None):
+        op("s", lambda: g.scalar.activation(out[0], x[0], F.Copy, scale=scale), [out], [x], grp=grp)
+
+    def mx(bank, left, la, right, a, b, pre=()):
+        out = V("ps", 512 * bank, 512 * bank + b - a)
+        lq, ls, rq, rs = V("q" + left, la, la + 128), V("s" + left, la, la + 128), V("q" + right, a, b), V("s" + right, a, b)
+        op("t", lambda: g.tensor.matmul_mx(out[0], lq[0], ls[0], rq[0], rs[0], True, True), [out], [lq, ls, rq, rs], pre=pre)
+
+    def iota(out, pat, base=0, cm=0, exact=False):
+        if exact:
+            op("g", lambda: g.iota(out[0], pat, base, cm), [out], [])
+        else:
+            op("g", lambda: g.iota(out[0], pat, base, cm, allow_small_or_imprecise_dtypes=True), [out], [])
+
+    def sel(out, x, pat, cmp, fl, base, cm):
+        op("g", lambda: g.affine_select(out[0], x[0], pat, cmp, fl, base, cm), [out], [x])
+
+    def load(out, src, codes=False, q="y", grp=None):
+        ap = out[0].bitcast(dt.uint8) if codes else out[0]
+        op(q, lambda: queues[q].dma_start(ap, a_(src)), [out], [src], kind="dma", grp=grp)
+
+    def store(q, dst, x, ap=None):
+        op(q, lambda: queues[q].dma_start(dst, x[0] if ap is None else ap), [], [x], kind="store")
+
+    def P(bank, n):
+        return V("ps", 512 * bank, 512 * bank + n)
+
+    def col(k):
+        return V("cl", k, k + 1)
+
+    def cand(i):
+        return V("qq", 16 * i + E0, 2376, 112)
+
+    def plane(t, a=0, b=416):
+        return V("yd", 416 * t + a, 416 * t + b)
+
+    def twins(t):
+        for k in (1, 2):
+            load(V("xx", 4 * C * k, 4 * C * k + 4 * C), V("xx", 0, 4 * C), grp="tw%d" % t)
+
+    RC, QC, NR, NQ, MQ, R21, PQ, LT, AL, BE, CZ, CE, CS, R4, TQ, N4, N3, N2, N1 = range(19)
+    H = C // 2
+
+    load(V("ut"), T.u[:])
+    load(V("xx", 0, 4 * H), T.x[:, 0:4 * H])
+    load(V("xx", 4 * H, 4 * C), T.x[:, 4 * H:4 * C])
+    twins(0)
+    load(V("qw"), T.wc[:], codes=True)
+    load(V("sw"), T.ws[:])
+    load(V("vt"), T.v[:])
+
+    iota(V("ci", 0, 1), [[0, 1]], 0, 1, exact=True)
+    fill(V("wr"), 0.0)
+    fill(V("unit"), U)
+    fill(V("wf"), 0.0)
+    iota(V("xm4"), [[0, 20], [1, 4]])
+    iota(V("n16"), [[16, 21]])
+    iota(V("n1"), [[1, 21]])
+    for i in range(4):
+        sel(V("wr"), V("wr"), [[-16, 8], [0, 4]], A.not_equal, float(8 >> i), -i, 1)
+    sel(V("bd"), V("unit"), [[-16, 8], [0, 16]], A.is_ge, 0.0, 0, 1)
+    iota(V("mc0"), [[1, 16], [0, 21]])
+    ts(V("ci", 1, 2), V("ci", 0, 1), 15, A.bitwise_and)
+    ts(V("ci", 2, 3), V("ci", 0, 1), 2, A.logical_shift_right, 3, A.bitwise_and)
+    ts(V("ci", 3, 4), V("ci", 0, 1), 3, A.bitwise_and)
+    fill(V("wi"), 0.0)
+    cp(V("cl", RC, RC + 2), V("ci", 1, 3))
+    cp(col(R4), V("ci", 3, 4))
+    fill(V("oh"), 0.0)
+    ts(V("cl", NR, NR + 2), V("cl", RC, RC + 2), -1.0, A.mult)
+    ts(V("tl", 0, 21), V("n16"), col(RC), A.add)
+    ts(col(R21), col(RC), 21.0, A.mult)
+    fill(V("st", C, 512), 0.0)
+    ts(V("tl", 21, 42), V("tl", 0, 21), 1.0 / 21, A.mult, 0.5 / 21 - 0.5, A.add)
+    ts(V("ltr", 0, 21), V("n1"), col(R21), A.add)
+    cp(V("tli", 0, 21), V("tl", 21, 42))
+    ts(V("lt4", 0, 21), V("n1"), col(R21), A.add, 4.0, A.mult)
+    ts(V("tl", 42, 63), V("tli", 0, 21), -21.0, A.mult)
+    fill(V("fs", 80, 84), 0.0)
+    tt(V("tl", 21, 42), V("tl", 42, 63), V("tl", 0, 21), A.add)
+    fill(V("rst"), 1.0)
+    ts(V("loh", 0, 21), V("tl", 21, 42), 4.0, A.mult, 3.0, A.add)
+    fill(V("rst", 0, 168, 21), 0.0)
+    act(col(MQ), col(QC), 16.0, -48.0)
+    act(V("df"), V("xm4"), 1.0, col(NQ), F.Abs)
+    act(col(N4), col(QC), -256.0 * U, (16 * 48 + B0 + 256 + 16) * U)
+    act(V("df"), V("df"), 1.0, 0.0, F.Sign)
+    for v, k in ((3, N3), (2, N2), (1, N1)):
+        act(col(k), col(QC), -16.0 * 2.0 ** (v - 4), 48.5 * 2.0 ** (v - 4) - 0.5)
+    act(V("df"), V("df"), -1040.0, 1024.0)
+    for t in range(4):
+        acp(V("wf", 5 * t, 512, 16), V("wr"), grp="wf")
+    act(V("hh"), V("oh", 0, 800), 1.0, EMPTY)
+    act(V("mc"), V("mc0"), 1.0, col(MQ))
+    act(V("mc", 20, 336, 21), V("mc0", 20, 336, 21), 0.0, -999.0)
+    sel(V("bd"), V("bd"), [[16, 8], [0, 16]], A.is_ge, 0.0, 15, -1)
+    sel(V("wi", 0, 512, 4), V("bd"), [[1, 128]], A.is_ge, 0.0, 0, -1)
+    sel(V("wi", 1, 512, 4), V("bd"), [[-1, 128]], A.is_gt, 0.0, 0, 1)
+    iota(V("six"), [[0, 16]], 6)
+    iota(V("s4"), [[4, 80]])
+    iota(V("jv"), [[1, C]], C)
+    iota(V("gap"), [[0, 16]])
+    iota(V("dd"), [[0, 16]], -1)
+    iota(V("six", 0, 1), [[0, 1]])
+    iota(V("sk0"), [[-16, 6], [16, 16]], B0 + 22)
+    iota(V("d5"), [[0, 96]])
+    iota(V("x16"), [[0, 20], [1, 16]])
+    iota(V("d5", 0, 96, 16), [[0, 6]], -65536)
+    iota(V("d5", 15, 96, 16), [[16, 6]])
+    iota(V("bt", 4 * L, 512), [[0, 128]])
+    X4 = V("xm4", 0, 4)
+    ts(col(TQ), col(QC), -1.0, A.mult, 5.0, A.add)
+    ts(col(LT), col(QC), 3.0, A.is_lt)
+    ts(V("c4", 0, 4), X4, col(QC), A.is_equal)
+    ts(col(PQ), col(QC), 1.0, A.add, col(TQ), A.min)
+    fill(V("rs2"), 0.0)
+    ts(V("c4", 4, 8), X4, col(PQ), A.is_equal)
+    fill(V("rs2", 0, 336, 2), -4.0)
+    fill(V("vd"), 0.0)
+    fill(cand(6), 1.0)
+    fill(V("vd", 0, 147, 7), 1.0)
+    quant("u", 0, 128, V("ut"))
+    act(V("rs3"), V("rs2"), 0.25, 1.0)
+    act(col(AL), col(LT), 8192.0 - 640.0, 640.0)
+    act(col(BE), col(LT), -8192.0 - 640.0, 8192.0)
+    act(col(CZ), col(LT), 2560.0, -1280.0)
+    act(V("c4", 8, 12), V("c4", 4, 8), -4096.0, 4096.0)
+    act(V("c4", 16, 20), V("c4", 0, 4), col(AL))
+    act(V("c4", 20, 24), V("c4", 4, 8), col(BE))
+    act(V("c4", 12, 16), V("c4", 8, 12), 1.0, col(QC))
+    act(col(CZ), col(CZ), 1.0, col(R4))
+    act(col(CS), col(RC), -1024.0, 15360.0)
+    act(col(CE), col(RC), -1024.0, 15360.0 - C)
+
+    def late_constants(stage):
+        if stage == 0:
+            quant("f", 0, 128, V("wf"))
+        if stage == 1:
+            quant("i", 0, 128, V("wi"))
+        if stage == 7:
+            tt(V("c4", 0, 4), V("c4", 16, 20), V("c4", 20, 24), A.add)
+            ts(V("lrep"), V("six", 2, 8), 0.0, A.mult, col(RC), A.add)
+        if stage == 2:
+            for x in range(4):
+                act(V("mm", x, C, 4), V("s4"), 1.0, V("c4", 12 + x, 13 + x), grp="mm")
+                act(V("dm", x, C, 4), V("s4"), 0.0, V("c4", x, x + 1), grp="dm")
+            act(V("sk"), V("sk0"), 1.0, col(NR))
+        if stage == 3:
+            act(V("dw"), V("x16"), 1.0, col(NR), F.Abs)
+            act(V("dw"), V("dw"), 1.0, 0.0, F.Sign)
+            act(V("dw"), V("dw"), -66560.0, 65536.0)
+        if stage == 4:
+            fill(V("eb"), 0.0)
+            fill(V("ones"), 1.0)
+            fill(V("zer"), 0.0)
+            sel(V("eb", 3, 515, 4), V("ones"), [[-1, 128]], A.is_equal, 0.0, 0, 1)
+            quant("a0", L, 224, V("zer"))
+            iota(V("tb0"), [[1, 50], [0, 16]], -(B0 // 16) - 1)
+        if stage == 5:
+            for b in range(4):
+                quant("e", 128 * b, 128 * b + 128, V("eb", 3 - b, 515 - b))
+        if stage == 6:
+            quant("v", 0, 128, V("vt"))
+            ts(V("tb"), V("tb0"), -1.0, A.max)
+
+    for t in range(R):
+        first = t == 0
+        G = lambda s: "%s%d" % (s, t)
+        for h in range(2):
+            quant("x", H * h, H * h + H, V("xx", 4 * H * h, 4 * H * h + 4 * H))
+            mx(h, "u", 0, "x", H * h, H * h + H)
+        if first:
+            late_constants(0)
+        for h in range(2):
+            ts(V("st", H * h, H * h + H), P(h, H), 0.0, A.is_ge, grp=G("st"))
+        quant("s", 0, 128, V("st"))
+        mx(2, "f", 0, "s", 0, 128)
+        if first:
+            late_constants(1)
+        scan(V("fs", 0, 80), V("df"), P(2, 80), A.add, A.min)
+        tt(V("oh", 0, 1344, 4), I(V("fs"), V("loh", 0, 21)), V("mc"), A.is_equal)
+        leaf = V("fs", 3, 84, 4)
+        for v, k in ((3, N3), (2, N2), (1, N1)):
+            act(V("nt0", 21 * (3 - v), 21 * (4 - v)), leaf, 2.0 ** (v - 4), col(k), grp=G("n0"))
+        act(V("nt", 0, 21), leaf, 16.0 * U, col(N4))
+        act(V("nt0"), V("nt0"), 1.0, MAGIC)
+        cp(V("oh", 5, 672, 4), V("oh", 0, 668, 4))
+        cp(V("oh", 677, 1344, 4), V("oh", 672, 1340, 4))
+        for h in range(2):
+            quant("o", 168 * h, 168 * h + 168, V("oh", 672 * h, 672 * h + 672))
+            mx(3 + h, "i", 0, "o", 168 * h, 168 * h + 168)
+        act(V("k4"), I(V("oh"), V("lt4", 0, 21)), 2064.0 * U, -16.0 * U)
+        for v in (3, 2, 1):
+            act(V("nt", 21 * (4 - v), 21 * (5 - v)), V("nt0", 21 * (3 - v), 21 * (4 - v)), 16.0 * U,
+                (B0 + (16 << v) + 16 - 16 * MAGIC) * U)
+        if first:
+            late_constants(7)
+        for h in range(2):
+            scan(V("cnt", 168 * h, 168 * h + 168), V("rst"), P(3 + h, 168), A.mult, A.add, grp=G("cnt"))
+        ts(V("t4", 0, 192), I(V("cnt"), V("ltr", 0, 12)), OFF[4] * U, A.add, grp=G("t4"))
+        act(V("t4", 192, 336), I(V("cnt"), V("ltr", 12, 21)), 1.0, OFF[4] * U, grp=G("t4"))
+        if first:
+            late_constants(2)
+        act(V("inv"), V("jv"), 1.0, -float(C))
+        way, cur = V("k4"), V("t4")
+        for v in (4, 3, 2, 1):
+            n, st = 21 << v, 112 >> v
+            end = 16 * (v + 1) + E0
+            ts(V("r%d" % v), cur, (OFF[v] + 10) * U, A.max, (OFF[v - 1] / 2 - OFF[v] - 10) * U, A.add)
+            scan(V("qq", end - st * ((1 << v) - 1), end + 112 * 20 + 1, st), way, cur, A.add, A.min)
+            if v == 1:
+                tt(cand(1), V("r1", 0, n, 2), V("r1", 1, n, 2), A.add)
+            else:
+                scan(V("t%d" % (v - 1)), V("rs3", 0, n), V("r%d" % v), A.mult, A.add)
+                cur = V("t%d" % (v - 1), 1, n, 2)
+                scan(V("k%d" % (v - 1)), V("rs2", 0, n), way, A.add, A.max)
+                way = V("k%d" % (v - 1), 1, n, 2)
+            if v < 4:
+                tt(V("vd", v + 2, 147, 7), cand(v + 2), V("nt", 21 * (3 - v), 21 * (4 - v)), A.is_lt, grp=G("vd"))
+        ts(V("vd", 1, 147, 7), cand(1), (B0 + 32) * U, A.is_lt, grp=G("vd"))
+        ts(cand(0), cand(1), -(OFF[0] + 11) * U, A.add, grp=G("vd"))
+        tt(V("vd", 2, 147, 7), cand(2), V("nt", 63, 84), A.is_lt, grp=G("vd"))
+        scan(V("fin"), V("vd"), V("qq", E0, 2376, 16), A.add, A.min)
+        act(V("gap", 8, 9), V("t3", 321, 322), -1.0 / U, float(OFF[3] + 10), F.Relu, grp=G("gap"))
+        act(V("gap", 4, 8), V("t2", 161, 168, 2), -1.0 / U, float(OFF[2] + 10), F.Relu, grp=G("gap"))
+        act(V("gap", 2, 4), V("t1", 81, 84, 2), -1.0 / U, float(OFF[1] + 10), F.Relu, grp=G("gap"))
+        act(V("gap", 0, 1), V("qq", 2240 + 16 + E0, 2241 + 16 + E0), -1.0 / U, float(B0 + 22 + OFF[0] + 10), grp=G("gap"))
+        if first:
+            late_constants(3)
+        place = V("fin", 5, 140, 7)
+        scan(V("dd", 0, 9), V("six", 0, 9), V("gap", 0, 9), A.add, A.add)
+        ts(V("lpos"), place, 1.0 / U, A.mult)
+        ts(V("pos"), place, 1.0 / U, A.mult, 240.0, A.add)
+        scatter(V("hh"), V("lpos"), V("jv"))
+        ts(V("pa"), V("pos"), 1, A.logical_shift_right, 0xFFF0, A.bitwise_and)
+        tt(V("fl"), I(V("dd"), V("lrep")), V("sk"), A.is_ge)
+        tt(V("pc"), V("pos"), V("pa"), A.subtract)
+        tt(V("fd"), I(V("dd"), V("lrep")), V("fl"), A.mult)
+        ts(V("lpp"), V("pc"), 16.0, A.add, float(B0), A.max)
+        scan(V("fm"), V("d5"), V("fd"), A.add, A.max)
+        if t == R - 1:
+            acp(V("obf"), I(V("tb"), V("lpos")))
+            store("y", T.ob[:], V("obf"), T.obf[0:128:16, :])
+        tt(V("gg"), I(V("hh"), V("lpp")), V("mm"), A.min)
+        ts(V("lfix"), V("fm", 15, 96, 16), col(RC), A.add)
+        scan(V("gs"), V("dm"), V("gg"), A.add, A.min)
+        acp(V("ge"), I(V("hh"), V("lfix")))
+        ts(V("lm"), V("gs", 3, C, 4), 4.0, A.mult, col(CZ), A.add)
+        for (a, b, bank) in ((0, CUT, 4), (CUT, C, 0)):
+            tt(V("zt", 4 * a, 4 * b), I(V("xx", 4 * C, 12 * C), V("lm", a // 4, b // 4)), V("xx", 4 * a, 4 * b), A.add)
+            if a == 0:
+                scan(V("es"), V("dw", 0, L), V("ge"), A.add, A.min)
+            else:
+                ts(V("le"), V("es", 15, L, 16), col(CE), A.add)
+            quant("z", a, b, V("zt", 4 * a, 4 * b))
+            for k in range(4):
+                mx(bank + k, "w", 128 * k, "z", a, b)
+                acp(plane(k, a, b), P(bank + k, b - a), 0.015625, grp=G("ya") if a == 0 else None)
+        for k in range(3):
+            cp(V("bt", k, 4 * L, 4), I(plane(k, 0, C), V("le")), grp=G("bt"))
+        acp(V("bt", 3, 4 * L, 4), I(plane(3, 0, C), V("le")), grp=G("bt"))
+        qb, sb, qa, sa = G("qb"), G("sb"), G("qa"), G("sa")
+        quant(G("b"), 0, 128, V("bt"))
+        arr = T.sem[G("arr")]
+        op("g", lambda qa=qa, qb=qb, arr=arr: g.remote_dma(T[qa][:, 0:L].bitcast(dt.uint8), T[qb][:, 0:L].bitcast(dt.uint8),
+                                                          arr, T.sem.sent, pid, rid, mask), [], [V(qb)], kind="remote")
+        op("g", lambda sa=sa, sb=sb, arr=arr: g.remote_dma(T[sa][:, 0:L], T[sb][:, 0:L],
+                                                          arr, T.sem.sent, pid, rid, mask), [], [V(sb)], kind="remote")
+        if first:
+            late_constants(4)
+        scatter(V("inv"), V("le"), V("jv", 0, L))
+        if t + 1 < R:
+            quant("a%d" % (t + 1), L, 224, V("zer"))
+        scan(V("ivs"), V("dw"), V("inv"), A.add, A.min)
+        if t + 1 < R:
+            fill(V("hh", B0, B0 + 256), EMPTY)
+        ts(V("lsrc"), V("ivs", 15, C, 16), col(CS), A.add)
+        if first:
+            late_constants(5)
+        if t == 1:
+            late_constants(6)
+        for k in (1, 0, 3, 2):
+            mx(4 + k, "e", 128 * k, G("a"), 0, 128, pre=[(arr, 2 * n_in)] if k == 1 else [])
+        for k in range(4):
+            move = cp if k % 2 == 0 else acp
+            move(plane(k, C, 416), P(4 + k, L))
+            move(V("xx", k, 4 * C, 4), I(plane(k), V("lsrc")), grp=G("xx"))
+        if t + 1 < R:
+            twins(t + 1)
+
+    for h in range(2):
+        quant("x", H * h, H * h + H, V("xx", 4 * H * h, 4 * H * h + 4 * H))
+        mx(h, "v", 0, "x", H * h, H * h + H)
+        store("y", T.oc[:, 4 * H * h:4 * H * h + 4 * H], V("qx", H * h, H * h + H), T.qx[:, H * h:H * h + H].bitcast(dt.uint8))
+    for k in range(4):
+        store("y", T.osc[4 * k:4 * k + 4, :], V("sx"), T.sx[32 * k:32 * k + 4, :])
+    acp(V("yo", 0, H), P(0, H))
+    cp(V("yo", H, C), P(1, H))
+    store("s", T.y[:, 0:H], V("yo", 0, H))
+    store("s", T.y[:, H:C], V("yo", H, C))
+    emit(ops, queues, T)
+    g.wait_ge(T.sem.sent, 2 * R * n_out)

@@ -1,35 +1,36 @@
 import numpy as np
 from concourse.mybir import dt, AluOpType, ActivationFunctionType
+from concourse.bass import DstId, RemoteDMATransfer
 
 A = AluOpType
 F = ActivationFunctionType
 C, L, R = 320, 96, 3
 TD = "float16"
 U = 2.0 ** -11
-B0 = 288
-OFF = {v: B0 + 32 * (1 << v) - 11 for v in range(5)}
+OWN = 1024
+P0, B0 = 2, 262
+TAB = 592
 EMPTY = 2048.0
-MAGIC = 12582912.0
 CUT = 192
-E0 = 36
+E0 = 28
+PL = (0, 832, 416, 1248)
 Q4, U8, BF, F32, I32, U16 = "float8_e4m3fn_x4", "uint8", "bfloat16", "float32", "int32", "uint16"
 
 SCRATCH = {"ps": ("psum", [128, 4096], F32)}
 for _d, _list in (
-        (BF, "xx 3840 ut 512 vt 512 st 512 oh 1344 wf 512 wi 512 eb 516 zer 512 ones 128 unit 128 bd 128 wr 32 zt 1280 yd 1664 bt 512"),
-        (Q4, "qw 512 qu 128 qv 128 qx 320 qz 320 qs 128 qo 336 qf 128 qi 128 qe 512 qb0 128 qb1 128 qb2 128 qa0 224 qa1 224 qa2 224"),
-        (U8, "sw 512 su 128 sv 128 sx 320 sz 320 ss 128 so 336 sf 128 si 128 se 512 sb0 128 sb1 128 sb2 128 sa0 224 sa1 224 sa2 224"),
-        (F32, "cl 24 c4 24 mc0 336 mc 336 xm4 80 df 80 n16 21 n1 21 tl 64 rst 168 jv 320 s4 80 mm 320 x16 320 dw 320 sk0 96 sk 96 "
-              "d5 96 six 16 tb0 800 tb 800 obf 320 fs 84 nt0 63 nt 84 cnt 336 hh 800 gap 16 dd 16 fl 96 fd 96 fm 96 ge 96 es 96 "
-              "inv 320 ivs 320 yo 320"),
-        (TD, "rs2 336 rs3 336 dm 320 k4 336 k3 336 k2 168 k1 84 t4 336 t3 336 t2 168 t1 84 r4 336 r3 168 r2 84 r1 42 qq 2376 "
-             "vd 147 fin 147 gg 320 gs 320"),
-        (I32, "ci 8 tli 24 pos 20 pa 20 pc 20"),
-        (U16, "loh 22 ltr 22 lt4 22 lrep 6 lpos 20 lpp 20 lm 80 lfix 6 le 6 lsrc 20")):
+        (BF, "xx 3840 ut 512 vt 512 st 512 oh 1352 wf 512 wi 516 eb 516 zer 512 ones 128 unit 128 bd 128 wr 32 zt 1280 yd 1664 bt 512"),
+        (Q4, "qw 512 qu 128 qv 128 qx 320 qz 320 qs 128 qo 338 qf 128 qi 384 qe 512 qb0 128 qb1 128 qb2 128 qa0 224 qa1 224 qa2 224"),
+        (U8, "sw 512 su 128 sv 128 sx 320 sz 320 ss 128 so 338 sf 128 si 384 se 512 sb0 128 sb1 128 sb2 128 sa0 224 sa1 224 sa2 224"),
+        (F32, "cl 32 c4 12 gc8 32 mc0 168 mc 336 xm4 80 xm8 80 df 80 n1 21 tl 64 rst 84 jm 640 jv2 192 sk0 96 sk 96 d8 320 "
+              "tb 592 obf 320 fs 84 cnt 336 hh 592 gsm 24 gr 96 dd 96 ns 96 hw 96 ge 96 es 96 inv 736 ivs 320 yo 320"),
+        (TD, "m2 336 m16 336 dm 320 tx 336 r4 336 r3 168 r2 84 r1 42 aq 1712 tn 100 of1 100 of2 100 thr 100 vd 100 cd 200 fin 200 "
+             "gg 320 gs 320"),
+        (I32, "ci 8 tli 24"),
+        (U16, "loh 22 ltr 22 lrep 6 lp 40 lm 80 lfix 6 le 12 lsrc 40")):
     _w = _list.split()
     for _k in range(0, len(_w), 2):
         SCRATCH[_w[_k]] = ("sbuf", [128, int(_w[_k + 1])], _d)
-NS = 100
+NS = 110
 SEMAPHORES = ["s%d" % i for i in range(NS)] + ["arr0", "arr1", "arr2", "sent", "stored"]
 
 
@@ -47,7 +48,7 @@ def emit(ops, queues, T):
         mine = []
         for k in range(i - 1, -1, -1):
             e = ops[k]
-            if k in known[o["q"]] or e["kind"] in ("remote", "store"):
+            if k in known[o["q"]] or e["kind"] in ("remote", "store") or (o["acc"] and e["acc"] == o["acc"]):
                 continue
             if meet(o["w"], e["w"] + e["r"]) or meet(o["r"], e["w"]) or (e["q"] != o["q"] and meet(o["r"], e["r"], "ps")):
                 key = e["grp"] or k
@@ -130,14 +131,14 @@ def rank_program(g, core, T, topo):
     def I(win, off):
         return (win[0].indirect(off[0]), win[1] + off[1])
 
-    def op(q, f, w, r, kind="c", pre=(), grp=None):
+    def op(q, f, w, r, kind="c", pre=(), grp=None, acc=None):
         ww, rr = [], []
         for x in w:
             ww += x[1]
         for x in r:
             if isinstance(x, tuple):
                 rr += x[1]
-        ops.append({"q": q, "f": f, "w": ww, "r": rr, "kind": kind, "pre": list(pre), "grp": grp})
+        ops.append({"q": q, "f": f, "w": ww, "r": rr, "kind": kind, "pre": list(pre), "grp": grp, "acc": acc})
 
     def a_(x):
         return x[0] if isinstance(x, tuple) else x
@@ -171,12 +172,13 @@ def rank_program(g, core, T, topo):
         op("s", lambda: g.scalar.activation(out[0], x[0], f, bias=a_(bias), scale=a_(scale)), [out], [x, scale, bias], grp=grp)
 
     def acp(out, x, scale=1.0, grp=None):
-        op("s", lambda: g.scalar.activation(out[0], x[0], F.Copy, scale=scale), [out], [x], grp=grp)
+        op("s", lambda: g.scalar.activation(out[0], x[0], F.Copy, scale=a_(scale)), [out], [x, scale], grp=grp)
 
-    def mx(bank, left, la, right, a, b, pre=()):
+    def mx(bank, left, la, right, a, b, pre=(), start=True, stop=True, acc=None):
         out = V("ps", 512 * bank, 512 * bank + b - a)
         lq, ls, rq, rs = V("q" + left, la, la + 128), V("s" + left, la, la + 128), V("q" + right, a, b), V("s" + right, a, b)
-        op("t", lambda: g.tensor.matmul_mx(out[0], lq[0], ls[0], rq[0], rs[0], True, True), [out], [lq, ls, rq, rs], pre=pre)
+        op("t", lambda: g.tensor.matmul_mx(out[0], lq[0], ls[0], rq[0], rs[0], start, stop), [out], [lq, ls, rq, rs], pre=pre,
+           acc=acc, grp=acc)
 
     def iota(out, pat, base=0, cm=0, exact=False):
         if exact:
@@ -194,243 +196,237 @@ def rank_program(g, core, T, topo):
     def store(q, dst, x, ap=None):
         op(q, lambda: queues[q].dma_start(dst, x[0] if ap is None else ap), [], [x], kind="store")
 
-    def P(bank, n):
-        return V("ps", 512 * bank, 512 * bank + n)
+    def P(bank, n, a=0, step=1):
+        return V("ps", 512 * bank + a, 512 * bank + n, step)
 
     def col(k):
         return V("cl", k, k + 1)
 
-    def cand(i):
-        return V("qq", 16 * i + E0, 2376, 112)
+    def plane(k, a, b):
+        return V("yd", PL[k] + a, PL[k] + b)
 
-    def plane(t, a=0, b=416):
-        return V("yd", 416 * t + a, 416 * t + b)
+    def way(v):
+        st = 80 >> v
+        return V("aq", 16 * v + E0 - 80 + st, 16 * v + E0 + 80 * 19 + 1, st)
 
     def twins(t):
         for k in (1, 2):
             load(V("xx", 4 * C * k, 4 * C * k + 4 * C), V("xx", 0, 4 * C), grp="tw%d" % t)
 
-    RC, QC, NR, NQ, MQ, R21, PQ, LT, AL, BE, CZ, CE, CS, R4, TQ, N4, N3, N2, N1 = range(19)
+    GC, RC, QC, RH, NR, C2, R21, M0, M1, N4, N3, N2, N1, R4, R1, CZ, CE, TM = range(18)
     H = C // 2
 
-    load(V("ut"), T.u[:])
     load(V("xx", 0, 4 * H), T.x[:, 0:4 * H])
+    load(V("ut"), T.u[:], q="s")
     load(V("xx", 4 * H, 4 * C), T.x[:, 4 * H:4 * C])
-    twins(0)
     load(V("qw"), T.wc[:], codes=True)
     load(V("sw"), T.ws[:])
     load(V("vt"), T.v[:])
+    twins(0)
 
     iota(V("ci", 0, 1), [[0, 1]], 0, 1, exact=True)
-    fill(V("wr"), 0.0)
     fill(V("unit"), U)
-    fill(V("wf"), 0.0)
-    iota(V("xm4"), [[0, 20], [1, 4]])
-    iota(V("n16"), [[16, 21]])
-    iota(V("n1"), [[1, 21]])
-    for i in range(4):
-        sel(V("wr"), V("wr"), [[-16, 8], [0, 4]], A.not_equal, float(8 >> i), -i, 1)
-    sel(V("bd"), V("unit"), [[-16, 8], [0, 16]], A.is_ge, 0.0, 0, 1)
-    iota(V("mc0"), [[1, 16], [0, 21]])
-    ts(V("ci", 1, 2), V("ci", 0, 1), 15, A.bitwise_and)
-    ts(V("ci", 2, 3), V("ci", 0, 1), 2, A.logical_shift_right, 3, A.bitwise_and)
-    ts(V("ci", 3, 4), V("ci", 0, 1), 3, A.bitwise_and)
+    fill(V("c4", 0, 4), 2.0)
     fill(V("wi"), 0.0)
-    cp(V("cl", RC, RC + 2), V("ci", 1, 3))
-    cp(col(R4), V("ci", 3, 4))
-    fill(V("oh"), 0.0)
-    ts(V("cl", NR, NR + 2), V("cl", RC, RC + 2), -1.0, A.mult)
-    ts(V("tl", 0, 21), V("n16"), col(RC), A.add)
-    ts(col(R21), col(RC), 21.0, A.mult)
+    iota(V("xm4"), [[0, 20], [1, 4]])
+    iota(V("gc8"), [[1, 8], [0, 4]])
+    iota(V("n1"), [[1, 21]])
+    iota(V("mc0"), [[1, 4], [0, 21], [4, 2]])
+    sel(V("bd"), V("unit"), [[-16, 8], [0, 16]], A.is_ge, 0.0, 0, 1)
+    sel(V("wi", 2, 514, 4), V("wi", 2, 514, 4), [[1, 128]], A.not_equal, -OWN * U, 0, -1)
+    sel(V("bd"), V("bd"), [[16, 8], [0, 16]], A.is_ge, 0.0, 15, -1)
+    ts(V("ci", 1, 2), V("ci", 0, 1), 4, A.logical_shift_right, grp="ci")
+    ts(V("ci", 2, 3), V("ci", 0, 1), 15, A.bitwise_and, grp="ci")
+    ts(V("ci", 3, 4), V("ci", 0, 1), 2, A.logical_shift_right, 3, A.bitwise_and, grp="ci")
+    ts(V("ci", 4, 5), V("ci", 0, 1), 1, A.logical_shift_right, 7, A.bitwise_and, grp="ci")
+    fill(V("wf"), 0.0)
+    cp(V("cl", GC, GC + 4), V("ci", 1, 5))
     fill(V("st", C, 512), 0.0)
-    ts(V("tl", 21, 42), V("tl", 0, 21), 1.0 / 21, A.mult, 0.5 / 21 - 0.5, A.add)
-    ts(V("ltr", 0, 21), V("n1"), col(R21), A.add)
-    cp(V("tli", 0, 21), V("tl", 21, 42))
-    ts(V("lt4", 0, 21), V("n1"), col(R21), A.add, 4.0, A.mult)
-    ts(V("tl", 42, 63), V("tli", 0, 21), -21.0, A.mult)
-    fill(V("fs", 80, 84), 0.0)
-    tt(V("tl", 21, 42), V("tl", 42, 63), V("tl", 0, 21), A.add)
+    ts(V("c4", 4, 8), V("xm4", 0, 4), col(RC), A.is_equal, 1.0 / 128, A.mult)
+    ts(col(C2), col(RH), 4.0, A.mult, 3.0, A.add)
+    ts(V("df"), V("xm4"), col(QC), A.is_equal, 0.125, A.subtract)
+    scan(V("c4", 8, 12), V("c4", 0, 4), V("c4", 4, 8), A.mult, A.add)
+    ts(V("tl", 0, 21), V("n1"), 32.0, A.mult, col(C2), A.add)
+    fill(V("fs", 80, 84), 9.0)
+    ts(V("wr"), V("gc8"), col(GC), A.is_equal, V("c4", 11, 12), A.mult)
+    ts(V("tli", 0, 21), V("tl", 0, 21), 1.0 / 84, A.mult, -43.0 / 84, A.add)
+    fill(V("oh", 0, 680), 0.0)
+    ts(V("tl", 21, 42), V("tli", 0, 21), -84.0, A.mult)
+    fill(V("oh", 680, 1352), 0.0)
+    tt(V("tl", 42, 63), V("tl", 21, 42), V("tl", 0, 21), A.add)
     fill(V("rst"), 1.0)
-    ts(V("loh", 0, 21), V("tl", 21, 42), 4.0, A.mult, 3.0, A.add)
-    fill(V("rst", 0, 168, 21), 0.0)
-    act(col(MQ), col(QC), 16.0, -48.0)
-    act(V("df"), V("xm4"), 1.0, col(NQ), F.Abs)
-    act(col(N4), col(QC), -256.0 * U, (16 * 48 + B0 + 256 + 16) * U)
-    act(V("df"), V("df"), 1.0, 0.0, F.Sign)
-    for v, k in ((3, N3), (2, N2), (1, N1)):
-        act(col(k), col(QC), -16.0 * 2.0 ** (v - 4), 48.5 * 2.0 ** (v - 4) - 0.5)
-    act(V("df"), V("df"), -1040.0, 1024.0)
+    cp(V("loh", 0, 21), V("tl", 42, 63))
+    fill(V("rst", 0, 84, 21), 0.0)
+    act(col(M0), col(QC), 0.125, -0.375)
+    act(col(M1), col(QC), 0.125, -0.375 + 8.0 / 128)
     for t in range(4):
         acp(V("wf", 5 * t, 512, 16), V("wr"), grp="wf")
-    act(V("hh"), V("oh", 0, 800), 1.0, EMPTY)
-    act(V("mc"), V("mc0"), 1.0, col(MQ))
-    act(V("mc", 20, 336, 21), V("mc0", 20, 336, 21), 0.0, -999.0)
-    sel(V("bd"), V("bd"), [[16, 8], [0, 16]], A.is_ge, 0.0, 15, -1)
-    sel(V("wi", 0, 512, 4), V("bd"), [[1, 128]], A.is_ge, 0.0, 0, -1)
-    sel(V("wi", 1, 512, 4), V("bd"), [[-1, 128]], A.is_gt, 0.0, 0, 1)
-    iota(V("six"), [[0, 16]], 6)
-    iota(V("s4"), [[4, 80]])
-    iota(V("jv"), [[1, C]], C)
-    iota(V("gap"), [[0, 16]])
-    iota(V("dd"), [[0, 16]], -1)
-    iota(V("six", 0, 1), [[0, 1]])
-    iota(V("sk0"), [[-16, 6], [16, 16]], B0 + 22)
-    iota(V("d5"), [[0, 96]])
-    iota(V("x16"), [[0, 20], [1, 16]])
-    iota(V("d5", 0, 96, 16), [[0, 6]], -65536)
-    iota(V("d5", 15, 96, 16), [[16, 6]])
-    iota(V("bt", 4 * L, 512), [[0, 128]])
-    X4 = V("xm4", 0, 4)
-    ts(col(TQ), col(QC), -1.0, A.mult, 5.0, A.add)
-    ts(col(LT), col(QC), 3.0, A.is_lt)
-    ts(V("c4", 0, 4), X4, col(QC), A.is_equal)
-    ts(col(PQ), col(QC), 1.0, A.add, col(TQ), A.min)
-    fill(V("rs2"), 0.0)
-    ts(V("c4", 4, 8), X4, col(PQ), A.is_equal)
-    fill(V("rs2", 0, 336, 2), -4.0)
-    fill(V("vd"), 0.0)
-    fill(cand(6), 1.0)
-    fill(V("vd", 0, 147, 7), 1.0)
+    act(V("mc", 0, 168), V("mc0"), 1.0 / 128, col(M0), grp="mc")
+    act(V("mc", 168, 336), V("mc0"), 1.0 / 128, col(M1), grp="mc")
+    act(col(R21), col(RC), 21.0)
+    for v in (4, 3, 2, 1):
+        s = 2.0 ** (v - 4)
+        act(col(N4 + 4 - v), col(QC), -16.0 * s, 48.5 * s + (1 << v) + 1023.5, grp="nb")
+    sel(V("wi", 0, 512, 4), V("bd"), [[1, 128]], A.is_gt, 0.0, 0, -1)
+    sel(V("wi", 1, 512, 4), V("bd"), [[-1, 128]], A.is_ge, 0.0, 0, 1)
+    sel(V("wi", 0, 512, 4), V("wi", 0, 512, 4), [[1, 128]], A.not_equal, OWN * U, 0, -1)
     quant("u", 0, 128, V("ut"))
-    act(V("rs3"), V("rs2"), 0.25, 1.0)
-    act(col(AL), col(LT), 8192.0 - 640.0, 640.0)
-    act(col(BE), col(LT), -8192.0 - 640.0, 8192.0)
-    act(col(CZ), col(LT), 2560.0, -1280.0)
-    act(V("c4", 8, 12), V("c4", 4, 8), -4096.0, 4096.0)
-    act(V("c4", 16, 20), V("c4", 0, 4), col(AL))
-    act(V("c4", 20, 24), V("c4", 4, 8), col(BE))
-    act(V("c4", 12, 16), V("c4", 8, 12), 1.0, col(QC))
-    act(col(CZ), col(CZ), 1.0, col(R4))
-    act(col(CS), col(RC), -1024.0, 15360.0)
-    act(col(CE), col(RC), -1024.0, 15360.0 - C)
+    iota(V("hh"), [[0, TAB]], int(EMPTY))
+    iota(V("jm"), [[1, 640]])
+    iota(V("xm8"), [[0, 10], [1, 8]])
+    iota(V("sk0"), [[-16, 6], [10, 16]], B0)
+    iota(V("sk0", 0, 96, 16), [[0, 6]], -9999)
+    iota(V("sk0", 1, 96, 16), [[-16, 6]], P0)
+    iota(V("gsm"), [[0, 24]])
+    iota(V("gsm", 0, 4, 2), [[B0 + 8 - P0 - 10, 2]], P0 + 10)
+    iota(V("jv2"), [[1, L], [0, 2]], C)
+    iota(V("bt", 4 * L, 512), [[0, 128]])
+    iota(V("inv", 0, C), [[1, C]])
 
     def late_constants(stage):
         if stage == 0:
             quant("f", 0, 128, V("wf"))
         if stage == 1:
-            quant("i", 0, 128, V("wi"))
-        if stage == 7:
-            tt(V("c4", 0, 4), V("c4", 16, 20), V("c4", 20, 24), A.add)
-            ts(V("lrep"), V("six", 2, 8), 0.0, A.mult, col(RC), A.add)
+            fill(V("m2"), 1.0)
+            fill(V("m16"), 1.0)
         if stage == 2:
-            for x in range(4):
-                act(V("mm", x, C, 4), V("s4"), 1.0, V("c4", 12 + x, 13 + x), grp="mm")
-                act(V("dm", x, C, 4), V("s4"), 0.0, V("c4", x, x + 1), grp="dm")
-            act(V("sk"), V("sk0"), 1.0, col(NR))
+            for e in range(3):
+                quant("i", 128 * e, 128 * e + 128, V("wi", e, 512 + e))
+            act(V("tn", 0, 100, 5), V("n1", 0, 20), 0.0, (10240 + P0 - B0 - 10) / 10.0)
+            act(V("of2", 0, 100, 5), V("n1", 0, 20), 0.0, (-400 - OWN) * U)
+            act(V("of2", 1, 100, 5), V("n1", 0, 20), 0.0, (P0 - OWN + 10) * U)
         if stage == 3:
-            act(V("dw"), V("x16"), 1.0, col(NR), F.Abs)
-            act(V("dw"), V("dw"), 1.0, 0.0, F.Sign)
-            act(V("dw"), V("dw"), -66560.0, 65536.0)
+            ts(V("ltr", 0, 21), V("n1"), col(R21), A.add)
+            fill(V("m2", 0, 336, 2), 0.0)
+            fill(V("m16", 0, 336, 16), 0.0)
+            fill(V("thr"), OWN * U)
         if stage == 4:
+            fill(V("thr", 0, 100, 5), 2.0)
+            act(col(NR), col(RC), -1.0)
+            act(col(R4), col(QC), -4.0, col(RC))
+            act(col(R1), col(RH), -2.0, col(RC))
+            act(col(TM), col(QC), -2560.0, 7680.0)
+            for x in range(4):
+                act(V("dm", 80 * x, 80 * x + 80), V("df"), 3200.0, -240.0, grp="dm")
+            act(V("gsm", 16, 22), V("n1", 0, 6), -16.0, col(NR))
+            act(V("sk"), V("sk0"), 1.0, col(NR))
+            act(col(CZ), col(TM), 1.0, col(R4))
+            act(col(TM + 1), col(RH), -512.0, 3584.0)
+            act(col(CE), col(R1), 416.0, col(TM + 1))
+        if stage == 5:
+            ts(V("tl", 0, 6), V("n1", 1, 7), 1.0, A.mult)
+            ts(col(TM + 2), col(RC), 15.0, A.is_equal)
+        if stage == 6:
+            ts(V("lrep"), V("tl", 0, 6), col(TM + 2), A.mult, col(RC), A.add)
+        if stage == 7:
+            ts(V("xm8"), V("xm8"), col(RH), A.is_equal, 4608.0, A.mult)
+        if stage == 8:
+            for x in range(4):
+                act(V("d8", 80 * x, 80 * x + 80), V("xm8"), 1.0, -512.0, grp="d8")
+            act(plane(0, C, 416), V("sk"), 0.0)
+            act(plane(1, C, 416), V("sk"), 0.0)
+        if stage == 9:
             fill(V("eb"), 0.0)
             fill(V("ones"), 1.0)
-            fill(V("zer"), 0.0)
             sel(V("eb", 3, 515, 4), V("ones"), [[-1, 128]], A.is_equal, 0.0, 0, 1)
-            quant("a0", L, 224, V("zer"))
-            iota(V("tb0"), [[1, 50], [0, 16]], -(B0 // 16) - 1)
-        if stage == 5:
+        if stage == 10:
             for b in range(4):
                 quant("e", 128 * b, 128 * b + 128, V("eb", 3 - b, 515 - b))
-        if stage == 6:
+        if stage == 11:
             quant("v", 0, 128, V("vt"))
-            ts(V("tb"), V("tb0"), -1.0, A.max)
+            iota(V("tb", B0, B0 + 320), [[1, 32], [0, 10]], -1)
+            iota(V("tb", 0, B0 + 20), [[0, B0 + 20]], -1)
+            iota(V("tb", P0, P0 + 10), [[0, 10]])
+            iota(V("tb", B0 + 320, TAB), [[0, TAB - B0 - 320]])
 
     for t in range(R):
         first = t == 0
         G = lambda s: "%s%d" % (s, t)
+        late = late_constants if first else (lambda stage: None)
         for h in range(2):
             quant("x", H * h, H * h + H, V("xx", 4 * H * h, 4 * H * h + 4 * H))
             mx(h, "u", 0, "x", H * h, H * h + H)
-        if first:
-            late_constants(0)
+        late(0)
         for h in range(2):
             ts(V("st", H * h, H * h + H), P(h, H), 0.0, A.is_ge, grp=G("st"))
         quant("s", 0, 128, V("st"))
         mx(2, "f", 0, "s", 0, 128)
-        if first:
-            late_constants(1)
+        late(1)
         scan(V("fs", 0, 80), V("df"), P(2, 80), A.add, A.min)
-        tt(V("oh", 0, 1344, 4), I(V("fs"), V("loh", 0, 21)), V("mc"), A.is_equal)
-        leaf = V("fs", 3, 84, 4)
-        for v, k in ((3, N3), (2, N2), (1, N1)):
-            act(V("nt0", 21 * (3 - v), 21 * (4 - v)), leaf, 2.0 ** (v - 4), col(k), grp=G("n0"))
-        act(V("nt", 0, 21), leaf, 16.0 * U, col(N4))
-        act(V("nt0"), V("nt0"), 1.0, MAGIC)
-        cp(V("oh", 5, 672, 4), V("oh", 0, 668, 4))
-        cp(V("oh", 677, 1344, 4), V("oh", 672, 1340, 4))
-        for h in range(2):
-            quant("o", 168 * h, 168 * h + 168, V("oh", 672 * h, 672 * h + 672))
-            mx(3 + h, "i", 0, "o", 168 * h, 168 * h + 168)
-        act(V("k4"), I(V("oh"), V("lt4", 0, 21)), 2064.0 * U, -16.0 * U)
-        for v in (3, 2, 1):
-            act(V("nt", 21 * (4 - v), 21 * (5 - v)), V("nt0", 21 * (3 - v), 21 * (4 - v)), 16.0 * U,
-                (B0 + (16 << v) + 16 - 16 * MAGIC) * U)
-        if first:
-            late_constants(7)
-        for h in range(2):
-            scan(V("cnt", 168 * h, 168 * h + 168), V("rst"), P(3 + h, 168), A.mult, A.add, grp=G("cnt"))
-        ts(V("t4", 0, 192), I(V("cnt"), V("ltr", 0, 12)), OFF[4] * U, A.add, grp=G("t4"))
-        act(V("t4", 192, 336), I(V("cnt"), V("ltr", 12, 21)), 1.0, OFF[4] * U, grp=G("t4"))
-        if first:
-            late_constants(2)
-        act(V("inv"), V("jv"), 1.0, -float(C))
-        way, cur = V("k4"), V("t4")
+        tt(V("oh", 8, 1352, 4), I(V("fs"), V("loh", 0, 21)), V("mc"), A.is_equal)
+        late(2)
         for v in (4, 3, 2, 1):
-            n, st = 21 << v, 112 >> v
-            end = 16 * (v + 1) + E0
-            ts(V("r%d" % v), cur, (OFF[v] + 10) * U, A.max, (OFF[v - 1] / 2 - OFF[v] - 10) * U, A.add)
-            scan(V("qq", end - st * ((1 << v) - 1), end + 112 * 20 + 1, st), way, cur, A.add, A.min)
-            if v == 1:
-                tt(cand(1), V("r1", 0, n, 2), V("r1", 1, n, 2), A.add)
-            else:
-                scan(V("t%d" % (v - 1)), V("rs3", 0, n), V("r%d" % v), A.mult, A.add)
-                cur = V("t%d" % (v - 1), 1, n, 2)
-                scan(V("k%d" % (v - 1)), V("rs2", 0, n), way, A.add, A.max)
-                way = V("k%d" % (v - 1), 1, n, 2)
-            if v < 4:
-                tt(V("vd", v + 2, 147, 7), cand(v + 2), V("nt", 21 * (3 - v), 21 * (4 - v)), A.is_lt, grp=G("vd"))
-        ts(V("vd", 1, 147, 7), cand(1), (B0 + 32) * U, A.is_lt, grp=G("vd"))
-        ts(cand(0), cand(1), -(OFF[0] + 11) * U, A.add, grp=G("vd"))
-        tt(V("vd", 2, 147, 7), cand(2), V("nt", 63, 84), A.is_lt, grp=G("vd"))
-        scan(V("fin"), V("vd"), V("qq", E0, 2376, 16), A.add, A.min)
-        act(V("gap", 8, 9), V("t3", 321, 322), -1.0 / U, float(OFF[3] + 10), F.Relu, grp=G("gap"))
-        act(V("gap", 4, 8), V("t2", 161, 168, 2), -1.0 / U, float(OFF[2] + 10), F.Relu, grp=G("gap"))
-        act(V("gap", 2, 4), V("t1", 81, 84, 2), -1.0 / U, float(OFF[1] + 10), F.Relu, grp=G("gap"))
-        act(V("gap", 0, 1), V("qq", 2240 + 16 + E0, 2241 + 16 + E0), -1.0 / U, float(B0 + 22 + OFF[0] + 10), grp=G("gap"))
-        if first:
-            late_constants(3)
-        place = V("fin", 5, 140, 7)
-        scan(V("dd", 0, 9), V("six", 0, 9), V("gap", 0, 9), A.add, A.add)
-        ts(V("lpos"), place, 1.0 / U, A.mult)
-        ts(V("pos"), place, 1.0 / U, A.mult, 240.0, A.add)
-        scatter(V("hh"), V("lpos"), V("jv"))
-        ts(V("pa"), V("pos"), 1, A.logical_shift_right, 0xFFF0, A.bitwise_and)
-        tt(V("fl"), I(V("dd"), V("lrep")), V("sk"), A.is_ge)
-        tt(V("pc"), V("pos"), V("pa"), A.subtract)
-        tt(V("fd"), I(V("dd"), V("lrep")), V("fl"), A.mult)
-        ts(V("lpp"), V("pc"), 16.0, A.add, float(B0), A.max)
-        scan(V("fm"), V("d5"), V("fd"), A.add, A.max)
+            act(V("tn", v, 100, 5), V("fs", 3, 80, 4), 128.0 * 2.0 ** (v - 4), col(N4 + 4 - v), grp=G("tn"))
+        quant("o", 0, 170, V("oh", 0, 680))
+        quant("o", 170, 338, V("oh", 680, 1352))
+        for h in range(2):
+            a = 168 * h
+            mx(3 + h, "i", 0, "o", a + 2, a + 170, stop=False, acc=G("cn%d" % h))
+            mx(3 + h, "i", 128, "o", a, a + 168, start=False, stop=False, acc=G("cn%d" % h))
+            mx(3 + h, "i", 256, "o", a, a + 168, start=False, acc=G("cn%d" % h))
+        shift = (B0 - OWN + 10 - 10240) * U
+        act(V("of1"), V("tn"), 10.0 * U, shift)
+        for v in (2, 3, 4):
+            act(V("of2", v, 100, 5), V("tn", v - 1, 100, 5), 10.0 * U, shift, grp=G("of2"))
+        late(3)
+        for h in range(4):
+            scan(V("cnt", 84 * h, 84 * h + 84), V("rst"), P(3 + h // 2, 168, h % 2, 2), A.mult, A.add, grp=G("cnt"))
+        ts(V("r4", 160, 336), I(V("cnt"), V("ltr", 10, 21)), 10 * U, A.max, 10 * U, A.subtract, grp=G("r4"))
+        act(V("r4", 0, 160), I(V("cnt"), V("ltr", 0, 10)), 1.0, -10 * U, F.Relu, grp=G("r4"))
+        late(4)
+        for v, at in ((4, 0), (3, 152), (2, 228)):
+            n = 21 << v
+            scan(V("tx", at, at + n), V("m2", 0, n), V("r%d" % v), A.mult, A.add)
+            scan(way(v), V("m16", 0, 320, 16 >> v), V("r%d" % v, 0, 20 << v), A.mult, A.max)
+            ts(V("r%d" % (v - 1)), V("tx", at + 1, at + n, 2), 10 * U, A.max, 10 * U, A.subtract)
+            late(9 - v)
+        act(V("gsm", 3, 10), V("tx", 309, 322, 2), -1.0 / U, 10.0, F.Relu)
+        tt(V("aq", E0, 1601 + E0, 80), V("r1", 0, 42, 2), V("r1", 1, 42, 2), A.add)
+        scan(way(1), V("m16", 0, 320, 8), V("r1", 0, 40), A.mult, A.max)
+        act(V("gsm", 1, 2), V("aq", 1600 + E0, 1601 + E0), -1.0 / U)
+        acp(V("gr"), I(V("gsm"), V("lrep")))
+        late(8)
+        own = V("aq", E0, 1600 + E0, 16)
+        tt(V("vd"), own, V("thr"), A.is_lt)
+        tt(V("cd", 0, 100), own, V("of1"), A.add)
+        tt(V("cd", 100, 200), own, V("of2"), A.add)
+        scan(V("fin", 0, 100), V("vd"), V("cd", 0, 100), A.add, A.min, grp=G("fin"))
+        scan(V("fin", 100, 200), V("vd"), V("cd", 100, 200), A.add, A.min, grp=G("fin"))
+        ts(V("lp"), V("fin", 4, 200, 5), 1.0 / U, A.mult, 0.0, A.max)
+        scan(V("dd"), V("m16", 0, L), V("gr"), A.mult, A.add)
+        scatter(V("hh"), V("lp", 0, 20), V("jm", 0, C))
         if t == R - 1:
-            acp(V("obf"), I(V("tb"), V("lpos")))
+            acp(V("obf"), I(V("tb"), V("lp", 0, 20)))
             store("y", T.ob[:], V("obf"), T.obf[0:128:16, :])
-        tt(V("gg"), I(V("hh"), V("lpp")), V("mm"), A.min)
-        ts(V("lfix"), V("fm", 15, 96, 16), col(RC), A.add)
+        tt(V("ns"), V("dd"), V("sk"), A.is_lt)
+        tt(V("gg"), I(V("hh"), V("lp", 20, 40)), V("jm", C, 2 * C), A.min)
+        scan(V("hw"), V("gr"), V("ns"), A.add, A.mult)
         scan(V("gs"), V("dm"), V("gg"), A.add, A.min)
-        acp(V("ge"), I(V("hh"), V("lfix")))
+        ts(V("lfix"), V("hw", 15, L, 16), -1.0, A.mult, V("dd", 9, 10), A.add)
         ts(V("lm"), V("gs", 3, C, 4), 4.0, A.mult, col(CZ), A.add)
+        acp(V("ge"), I(V("hh"), V("lfix")))
+        if t + 1 < R:
+            iota(V("hh", B0 + 20, B0 + 160), [[0, 140]], int(EMPTY))
+        if first:
+            fill(V("zer"), 0.0)
         for (a, b, bank) in ((0, CUT, 4), (CUT, C, 0)):
             tt(V("zt", 4 * a, 4 * b), I(V("xx", 4 * C, 12 * C), V("lm", a // 4, b // 4)), V("xx", 4 * a, 4 * b), A.add)
             if a == 0:
-                scan(V("es"), V("dw", 0, L), V("ge"), A.add, A.min)
+                scan(V("es"), V("d8", 0, L), V("ge"), A.add, A.min)
             else:
-                ts(V("le"), V("es", 15, L, 16), col(CE), A.add)
+                ts(V("le"), V("es", 7, L, 8), col(CE), A.add)
             quant("z", a, b, V("zt", 4 * a, 4 * b))
             for k in range(4):
                 mx(bank + k, "w", 128 * k, "z", a, b)
-                acp(plane(k, a, b), P(bank + k, b - a), 0.015625, grp=G("ya") if a == 0 else None)
-        for k in range(3):
-            cp(V("bt", k, 4 * L, 4), I(plane(k, 0, C), V("le")), grp=G("bt"))
-        acp(V("bt", 3, 4 * L, 4), I(plane(3, 0, C), V("le")), grp=G("bt"))
+                if a == 0 or k % 2:
+                    acp(plane(k, a, b), P(bank + k, b - a), 0.015625)
+            if a:
+                if first:
+                    quant("a0", L, 224, V("zer"))
+                for k in (0, 2):
+                    ts(plane(k, a, b), P(bank + k, b - a), 0.015625, A.mult)
+        cp(V("bt", 0, 4 * L, 2), I(V("yd", 0, 736), V("le")), grp=G("bt"))
+        acp(V("bt", 1, 4 * L, 2), I(V("yd", 832, 1568), V("le")), grp=G("bt"))
         qb, sb, qa, sa = G("qb"), G("sb"), G("qa"), G("sa")
         quant(G("b"), 0, 128, V("bt"))
         arr = T.sem[G("arr")]
@@ -438,25 +434,23 @@ def rank_program(g, core, T, topo):
                                                           arr, T.sem.sent, pid, rid, mask), [], [V(qb)], kind="remote")
         op("g", lambda sa=sa, sb=sb, arr=arr: g.remote_dma(T[sa][:, 0:L], T[sb][:, 0:L],
                                                           arr, T.sem.sent, pid, rid, mask), [], [V(sb)], kind="remote")
-        if first:
-            late_constants(4)
-        scatter(V("inv"), V("le"), V("jv", 0, L))
+        late(9)
+        scatter(V("inv"), V("le"), V("jv2"))
         if t + 1 < R:
             quant("a%d" % (t + 1), L, 224, V("zer"))
-        scan(V("ivs"), V("dw"), V("inv"), A.add, A.min)
+        scan(V("ivs"), V("d8"), V("inv", 0, C), A.add, A.min)
+        late(10)
+        ts(V("lsrc"), V("ivs", 7, C, 8), col(CE), A.add)
         if t + 1 < R:
-            fill(V("hh", B0, B0 + 256), EMPTY)
-        ts(V("lsrc"), V("ivs", 15, C, 16), col(CS), A.add)
-        if first:
-            late_constants(5)
+            iota(V("inv", 0, C), [[1, C]])
         if t == 1:
-            late_constants(6)
-        for k in (1, 0, 3, 2):
-            mx(4 + k, "e", 128 * k, G("a"), 0, 128, pre=[(arr, 2 * n_in)] if k == 1 else [])
+            late_constants(11)
         for k in range(4):
-            move = cp if k % 2 == 0 else acp
-            move(plane(k, C, 416), P(4 + k, L))
-            move(V("xx", k, 4 * C, 4), I(plane(k), V("lsrc")), grp=G("xx"))
+            mx(4 + k, "e", 128 * k, G("a"), 0, 128, pre=[(arr, 2 * n_in)] if k == 0 else [])
+        for k in range(4):
+            (cp if k % 2 == 0 else acp)(plane(k, C, 416), P(4 + k, L))
+        cp(V("xx", 0, 4 * C, 2), I(V("yd", 0, 832), V("lsrc")), grp=G("xx"))
+        acp(V("xx", 1, 4 * C, 2), I(V("yd", 832, 1664), V("lsrc")), grp=G("xx"))
         if t + 1 < R:
             twins(t + 1)
 

@@ -18,7 +18,7 @@ Q4, U8, BF, F32, I32, U16 = "float8_e4m3fn_x4", "uint8", "bfloat16", "float32", 
 
 SCRATCH = {"ps": ("psum", [128, 4096], F32)}
 for _d, _list in (
-        (BF, "xx 3840 ut 512 vt 512 st 512 oh 1352 wf 512 wi 516 eb 516 zer 512 ones 128 unit 128 bd 128 wr 32 zt 1280 yd 1664 bt 512"),
+        (BF, "xx 3840 ut 512 vt 512 st 512 oh 1352 wf 512 wi 516 eb 516 zer 512 ones 128 dc 128 lo 128 hi 128 wr 32 zt 1280 zm 512 yd 1664 bt 512"),
         (Q4, "qw 512 qu 128 qv 128 qx 320 qz 320 qs 128 qo 338 qf 128 qi 384 qe 512 qb0 128 qb1 128 qb2 128 qa0 224 qa1 224 qa2 224"),
         (U8, "sw 512 su 128 sv 128 sx 320 sz 320 ss 128 so 338 sf 128 si 384 se 512 sb0 128 sb1 128 sb2 128 sa0 224 sa1 224 sa2 224"),
         (F32, "cl 32 c4 12 gc8 32 mc0 168 mc 336 xm4 80 xm8 80 df 80 n1 21 tl 64 rst 84 jm 640 jv2 192 sk0 96 sk 96 d8 320 "
@@ -98,7 +98,6 @@ def emit(ops, queues, T):
 
 def engine_mask(topo, src, dst):
     e = topo.engines(src, dst)
-    e = e[::len(e) // 8]
     m = 0
     for k in e:
         m |= 1 << k
@@ -213,7 +212,7 @@ def rank_program(g, core, T, topo):
         for k in (1, 2):
             load(V("xx", 4 * C * k, 4 * C * k + 4 * C), V("xx", 0, 4 * C), grp="tw%d" % t)
 
-    GC, RC, QC, RH, NR, C2, R21, M0, M1, N4, N3, N2, N1, R4, R1, CZ, CE, TM = range(18)
+    GC, RC, QC, RH, NR, C2, R21, M0, M1, N4, N3, N2, N1, R4, R1, CZ, CE, HI, TM = range(19)
     H = C // 2
 
     load(V("xx", 0, 4 * H), T.x[:, 0:4 * H])
@@ -225,38 +224,40 @@ def rank_program(g, core, T, topo):
     twins(0)
 
     iota(V("ci", 0, 1), [[0, 1]], 0, 1, exact=True)
-    fill(V("unit"), U)
+    fill(V("zer"), 0.0)
+    for a, b in ((0, 512), (512, 1024), (1024, 1352)):
+        load(V("oh", a, b), V("zer", 0, b - a), q="s", grp="oh")
     fill(V("c4", 0, 4), 2.0)
-    fill(V("wi"), 0.0)
     iota(V("xm4"), [[0, 20], [1, 4]])
     iota(V("gc8"), [[1, 8], [0, 4]])
     iota(V("n1"), [[1, 21]])
+    iota(V("dc"), [[1, 128]], 0, -1)
     iota(V("mc0"), [[1, 4], [0, 21], [4, 2]])
-    sel(V("bd"), V("unit"), [[-16, 8], [0, 16]], A.is_ge, 0.0, 0, 1)
-    sel(V("wi", 2, 514, 4), V("wi", 2, 514, 4), [[1, 128]], A.not_equal, -OWN * U, 0, -1)
-    sel(V("bd"), V("bd"), [[16, 8], [0, 16]], A.is_ge, 0.0, 15, -1)
     ts(V("ci", 1, 2), V("ci", 0, 1), 4, A.logical_shift_right, grp="ci")
     ts(V("ci", 2, 3), V("ci", 0, 1), 15, A.bitwise_and, grp="ci")
     ts(V("ci", 3, 4), V("ci", 0, 1), 2, A.logical_shift_right, 3, A.bitwise_and, grp="ci")
     ts(V("ci", 4, 5), V("ci", 0, 1), 1, A.logical_shift_right, 7, A.bitwise_and, grp="ci")
     fill(V("wf"), 0.0)
     cp(V("cl", GC, GC + 4), V("ci", 1, 5))
-    fill(V("st", C, 512), 0.0)
+    fill(V("wi", 512, 516), 0.0)
+    fill(V("wi", 3, 512, 4), 0.0)
     ts(V("c4", 4, 8), V("xm4", 0, 4), col(RC), A.is_equal, 1.0 / 128, A.mult)
     ts(col(C2), col(RH), 4.0, A.mult, 3.0, A.add)
     ts(V("df"), V("xm4"), col(QC), A.is_equal, 0.125, A.subtract)
     scan(V("c4", 8, 12), V("c4", 0, 4), V("c4", 4, 8), A.mult, A.add)
     ts(V("tl", 0, 21), V("n1"), 32.0, A.mult, col(C2), A.add)
-    fill(V("fs", 80, 84), 9.0)
+    fill(V("st", C, 512), 0.0)
     ts(V("wr"), V("gc8"), col(GC), A.is_equal, V("c4", 11, 12), A.mult)
     ts(V("tli", 0, 21), V("tl", 0, 21), 1.0 / 84, A.mult, -43.0 / 84, A.add)
-    fill(V("oh", 0, 680), 0.0)
+    act(col(NR), col(RC), -1.0)
+    act(col(HI), col(RC), -1.0, 15.0)
+    ts(V("wi", 2, 512, 4), V("dc"), 0.0, A.is_equal, -OWN * U, A.mult)
     ts(V("tl", 21, 42), V("tli", 0, 21), -84.0, A.mult)
-    fill(V("oh", 680, 1352), 0.0)
+    ts(V("hi"), V("dc"), col(HI), A.is_le, U, A.mult)
+    ts(V("lo"), V("dc"), col(NR), A.is_ge, U, A.mult)
     tt(V("tl", 42, 63), V("tl", 21, 42), V("tl", 0, 21), A.add)
-    fill(V("rst"), 1.0)
+    fill(V("fs", 80, 84), 9.0)
     cp(V("loh", 0, 21), V("tl", 42, 63))
-    fill(V("rst", 0, 84, 21), 0.0)
     act(col(M0), col(QC), 0.125, -0.375)
     act(col(M1), col(QC), 0.125, -0.375 + 8.0 / 128)
     for t in range(4):
@@ -267,9 +268,18 @@ def rank_program(g, core, T, topo):
     for v in (4, 3, 2, 1):
         s = 2.0 ** (v - 4)
         act(col(N4 + 4 - v), col(QC), -16.0 * s, 48.5 * s + (1 << v) + 1023.5, grp="nb")
-    sel(V("wi", 0, 512, 4), V("bd"), [[1, 128]], A.is_gt, 0.0, 0, -1)
-    sel(V("wi", 1, 512, 4), V("bd"), [[-1, 128]], A.is_ge, 0.0, 0, 1)
-    sel(V("wi", 0, 512, 4), V("wi", 0, 512, 4), [[1, 128]], A.not_equal, OWN * U, 0, -1)
+    sel(V("hi"), V("hi"), [[1, 128]], A.is_gt, 0.0, 0, -1)
+    sel(V("wi", 1, 512, 4), V("lo"), [[-1, 128]], A.is_ge, 0.0, 0, 1)
+    sel(V("wi", 0, 512, 4), V("hi"), [[1, 128]], A.not_equal, OWN * U, 0, -1)
+    for name, n in (("rst", 84), ("m2", 336), ("m16", 336)):
+        act(V(name), V("mc", 0, n), 0.0, 1.0)
+    act(V("thr"), V("mc", 0, 100), 0.0, OWN * U)
+    for name, n, st in (("rst", 84, 21), ("m2", 336, 2), ("m16", 336, 16)):
+        act(V(name, 0, n, st), V("mc", 0, n // st), 0.0)
+    act(V("thr", 0, 100, 5), V("mc", 0, 20), 0.0, 2.0)
+    act(V("tn", 0, 100, 5), V("n1", 0, 20), 0.0, (10240 + P0 - B0 - 10) / 10.0)
+    act(V("of2", 0, 100, 5), V("n1", 0, 20), 0.0, (-400 - OWN) * U)
+    act(V("of2", 1, 100, 5), V("n1", 0, 20), 0.0, (P0 - OWN + 10) * U)
     quant("u", 0, 128, V("ut"))
     iota(V("hh"), [[0, TAB]], int(EMPTY))
     iota(V("jm"), [[1, 640]])
@@ -287,22 +297,13 @@ def rank_program(g, core, T, topo):
         if stage == 0:
             quant("f", 0, 128, V("wf"))
         if stage == 1:
-            fill(V("m2"), 1.0)
-            fill(V("m16"), 1.0)
-        if stage == 2:
-            for e in range(3):
+            for e in (2, 1):
                 quant("i", 128 * e, 128 * e + 128, V("wi", e, 512 + e))
-            act(V("tn", 0, 100, 5), V("n1", 0, 20), 0.0, (10240 + P0 - B0 - 10) / 10.0)
-            act(V("of2", 0, 100, 5), V("n1", 0, 20), 0.0, (-400 - OWN) * U)
-            act(V("of2", 1, 100, 5), V("n1", 0, 20), 0.0, (P0 - OWN + 10) * U)
+        if stage == 2:
+            quant("i", 0, 128, V("wi", 0, 512))
         if stage == 3:
             ts(V("ltr", 0, 21), V("n1"), col(R21), A.add)
-            fill(V("m2", 0, 336, 2), 0.0)
-            fill(V("m16", 0, 336, 16), 0.0)
-            fill(V("thr"), OWN * U)
         if stage == 4:
-            fill(V("thr", 0, 100, 5), 2.0)
-            act(col(NR), col(RC), -1.0)
             act(col(R4), col(QC), -4.0, col(RC))
             act(col(R1), col(RH), -2.0, col(RC))
             act(col(TM), col(QC), -2560.0, 7680.0)
@@ -353,8 +354,9 @@ def rank_program(g, core, T, topo):
         mx(2, "f", 0, "s", 0, 128)
         late(1)
         scan(V("fs", 0, 80), V("df"), P(2, 80), A.add, A.min)
-        tt(V("oh", 8, 1352, 4), I(V("fs"), V("loh", 0, 21)), V("mc"), A.is_equal)
         late(2)
+        tt(V("oh", 8, 776, 4), I(V("fs"), V("loh", 0, 12)), V("mc", 0, 192), A.is_equal)
+        tt(V("oh", 776, 1352, 4), I(V("fs"), V("loh", 12, 21)), V("mc", 192, 336), A.is_equal)
         for v in (4, 3, 2, 1):
             act(V("tn", v, 100, 5), V("fs", 3, 80, 4), 128.0 * 2.0 ** (v - 4), col(N4 + 4 - v), grp=G("tn"))
         quant("o", 0, 170, V("oh", 0, 680))
@@ -404,27 +406,30 @@ def rank_program(g, core, T, topo):
         scan(V("gs"), V("dm"), V("gg"), A.add, A.min)
         ts(V("lfix"), V("hw", 15, L, 16), -1.0, A.mult, V("dd", 9, 10), A.add)
         ts(V("lm"), V("gs", 3, C, 4), 4.0, A.mult, col(CZ), A.add)
+        win = V("xx", 4 * C, 12 * C)
+        acp(V("zm"), I(win, V("lm", CUT // 4, C // 4)))
         acp(V("ge"), I(V("hh"), V("lfix")))
         if t + 1 < R:
             iota(V("hh", B0 + 20, B0 + 160), [[0, 140]], int(EMPTY))
+        tt(V("zt", 0, 4 * CUT), I(win, V("lm", 0, CUT // 4)), V("xx", 0, 4 * CUT), A.add)
+        tt(V("zt", 4 * CUT, 4 * CUT + 256), V("zm", 0, 256), V("xx", 4 * CUT, 4 * CUT + 256), A.add)
+        quant("z", 0, CUT, V("zt", 0, 4 * CUT))
+        tt(V("zt", 4 * CUT + 256, 4 * C), V("zm", 256, 512), V("xx", 4 * CUT + 256, 4 * C), A.add)
+        for k in range(4):
+            mx(4 + k, "w", 128 * k, "z", 0, CUT)
+        for k in (0, 1, 3):
+            acp(plane(k, 0, CUT), P(4 + k, CUT), 0.015625)
+        scan(V("es"), V("d8", 0, L), V("ge"), A.add, A.min)
+        quant("z", CUT, C, V("zt", 4 * CUT, 4 * C))
+        ts(V("le"), V("es", 7, L, 8), col(CE), A.add)
+        ts(plane(2, 0, CUT), P(6, CUT), 0.015625, A.mult)
+        for k in (1, 0, 3, 2):
+            mx(k, "w", 128 * k, "z", CUT, C)
         if first:
-            fill(V("zer"), 0.0)
-        for (a, b, bank) in ((0, CUT, 4), (CUT, C, 0)):
-            tt(V("zt", 4 * a, 4 * b), I(V("xx", 4 * C, 12 * C), V("lm", a // 4, b // 4)), V("xx", 4 * a, 4 * b), A.add)
-            if a == 0:
-                scan(V("es"), V("d8", 0, L), V("ge"), A.add, A.min)
-            else:
-                ts(V("le"), V("es", 7, L, 8), col(CE), A.add)
-            quant("z", a, b, V("zt", 4 * a, 4 * b))
-            for k in range(4):
-                mx(bank + k, "w", 128 * k, "z", a, b)
-                if a == 0 or k % 2:
-                    acp(plane(k, a, b), P(bank + k, b - a), 0.015625)
-            if a:
-                if first:
-                    quant("a0", L, 224, V("zer"))
-                for k in (0, 2):
-                    ts(plane(k, a, b), P(bank + k, b - a), 0.015625, A.mult)
+            quant("a0", L, 224, V("zer"))
+        for k in (0, 2):
+            ts(plane(k, CUT, C), P(k, C - CUT), 0.015625, A.mult)
+            acp(plane(k + 1, CUT, C), P(k + 1, C - CUT), 0.015625)
         cp(V("bt", 0, 4 * L, 2), I(V("yd", 0, 736), V("le")), grp=G("bt"))
         acp(V("bt", 1, 4 * L, 2), I(V("yd", 832, 1568), V("le")), grp=G("bt"))
         qb, sb, qa, sa = G("qb"), G("sb"), G("qa"), G("sa")
@@ -445,8 +450,8 @@ def rank_program(g, core, T, topo):
             iota(V("inv", 0, C), [[1, C]])
         if t == 1:
             late_constants(11)
-        for k in range(4):
-            mx(4 + k, "e", 128 * k, G("a"), 0, 128, pre=[(arr, 2 * n_in)] if k == 0 else [])
+        for k in (1, 0, 3, 2):
+            mx(4 + k, "e", 128 * k, G("a"), 0, 128, pre=[(arr, 2 * n_in)] if k == 1 else [])
         for k in range(4):
             (cp if k % 2 == 0 else acp)(plane(k, C, 416), P(4 + k, L))
         cp(V("xx", 0, 4 * C, 2), I(V("yd", 0, 832), V("lsrc")), grp=G("xx"))
@@ -459,10 +464,11 @@ def rank_program(g, core, T, topo):
         mx(h, "v", 0, "x", H * h, H * h + H)
         store("y", T.oc[:, 4 * H * h:4 * H * h + 4 * H], V("qx", H * h, H * h + H), T.qx[:, H * h:H * h + H].bitcast(dt.uint8))
     for k in range(4):
-        store("y", T.osc[4 * k:4 * k + 4, :], V("sx"), T.sx[32 * k:32 * k + 4, :])
-    acp(V("yo", 0, H), P(0, H))
+        store("ys"[k // 2], T.osc[4 * k:4 * k + 4, :], V("sx"), T.sx[32 * k:32 * k + 4, :])
+        if k == 1:
+            acp(V("yo", 0, H), P(0, H))
+            store("s", T.y[:, 0:H], V("yo", 0, H))
     cp(V("yo", H, C), P(1, H))
-    store("s", T.y[:, 0:H], V("yo", 0, H))
-    store("s", T.y[:, H:C], V("yo", H, C))
+    store("y", T.y[:, H:C], V("yo", H, C))
     emit(ops, queues, T)
     g.wait_ge(T.sem.sent, 2 * R * n_out)

@@ -18,15 +18,15 @@ Q4, U8, BF, F32, I32, U16 = "float8_e4m3fn_x4", "uint8", "bfloat16", "float32", 
 
 SCRATCH = {"ps": ("psum", [128, 4096], F32)}
 for _d, _list in (
-        (BF, "xx 3840 ut 512 vt 512 st 512 oh 1352 wf 512 wi 516 eb 516 zer 512 ones 128 dc 128 lo 128 hi 128 wr 32 zt 1280 zm 512 yd 1664 bt 512"),
+        (BF, "xx 3840 ut 512 vt 512 st 512 oh 1352 wf 512 wi 520 eb 520 zer 680 ones 128 dc 128 lo 128 hi 128 wr 32 zt 1280 zm 512 yd 1664 bt 512"),
         (Q4, "qw 512 qu 128 qv 128 qx 320 qz 320 qs 128 qo 338 qf 128 qi 384 qe 512 qb0 128 qb1 128 qb2 128 qa0 224 qa1 224 qa2 224"),
         (U8, "sw 512 su 128 sv 128 sx 320 sz 320 ss 128 so 338 sf 128 si 384 se 512 sb0 128 sb1 128 sb2 128 sa0 224 sa1 224 sa2 224"),
         (F32, "cl 32 c4 12 gc8 32 mc0 168 mc 336 xm4 80 xm8 80 df 80 n1 21 tl 64 rst 84 jm 640 jv2 192 sk0 96 sk 96 d8 320 "
-              "tb 592 obf 320 fs 84 cnt 336 hh 592 gsm 24 gr 96 dd 96 ns 96 hw 96 ge 96 es 96 inv 736 ivs 320 yo 320"),
-        (TD, "m2 336 m16 336 dm 320 tx 336 r4 336 r3 168 r2 84 r1 42 aq 1712 tn 100 of1 100 of2 100 thr 100 vd 100 cd 200 fin 200 "
+              "tb 592 obf 320 fs 84 cnt 344 hh 592 gsm 24 gr 96 dd 96 ns 96 hw 96 ge 96 es 96 inv 736 ivs 320 yo 320"),
+        (TD, "m16 336 dm 320 tx 160 r4 704 r3 1012 r2 2540 r1 420 aq 1712 tn 100 of1 100 of2 100 thr 100 vd 100 cd 200 fin 200 "
              "gg 320 gs 320"),
         (I32, "ci 8 tli 24"),
-        (U16, "loh 22 ltr 22 lrep 6 lp 40 lm 80 lfix 6 le 12 lsrc 40")):
+        (U16, "loh 22 ltr 24 lrep 6 lp 40 lm 80 lfix 6 le 12 lsrc 40")):
     _w = _list.split()
     for _k in range(0, len(_w), 2):
         SCRATCH[_w[_k]] = ("sbuf", [128, int(_w[_k + 1])], _d)
@@ -204,29 +204,30 @@ def rank_program(g, core, T, topo):
     def plane(k, a, b):
         return V("yd", PL[k] + a, PL[k] + b)
 
-    def way(v):
-        st = 80 >> v
+    def way(v, n):
+        st = 80 // n
         return V("aq", 16 * v + E0 - 80 + st, 16 * v + E0 + 80 * 19 + 1, st)
 
     def twins(t):
         for k in (1, 2):
             load(V("xx", 4 * C * k, 4 * C * k + 4 * C), V("xx", 0, 4 * C), grp="tw%d" % t)
 
-    GC, RC, QC, RH, NR, C2, R21, M0, M1, N4, N3, N2, N1, R4, R1, CZ, CE, HI, TM = range(19)
-    H = C // 2
+    GC, RC, QC, RH, HB, NR, C2, R21, M0, M1, N4, N3, N2, N1, R4, R1, CZ, CE, HI, TM = range(20)
+    runs = ((0, CUT), (CUT, C))
 
-    load(V("xx", 0, 4 * H), T.x[:, 0:4 * H])
     load(V("ut"), T.u[:], q="s")
-    load(V("xx", 4 * H, 4 * C), T.x[:, 4 * H:4 * C])
+    for a, b in runs:
+        load(V("xx", 4 * a, 4 * b), T.x[:, 4 * a:4 * b])
+
+    iota(V("ci", 0, 1), [[0, 1]], 0, 1, exact=True)
+    fill(V("zer"), 0.0)
+    for name, a, b in (("st", C, 512), ("oh", 0, 680), ("oh", 680, 1352), ("eb", 0, 520)):
+        load(V(name, a, b), V("zer", 0, b - a), grp="z" + name)
     load(V("qw"), T.wc[:], codes=True)
     load(V("sw"), T.ws[:])
     load(V("vt"), T.v[:])
     twins(0)
-
-    iota(V("ci", 0, 1), [[0, 1]], 0, 1, exact=True)
-    fill(V("zer"), 0.0)
-    for a, b in ((0, 512), (512, 1024), (1024, 1352)):
-        load(V("oh", a, b), V("zer", 0, b - a), q="s", grp="oh")
+    act(V("ones"), V("zer", 0, 128), 1.0, 1.0)
     fill(V("c4", 0, 4), 2.0)
     iota(V("xm4"), [[0, 20], [1, 4]])
     iota(V("gc8"), [[1, 8], [0, 4]])
@@ -237,49 +238,47 @@ def rank_program(g, core, T, topo):
     ts(V("ci", 2, 3), V("ci", 0, 1), 15, A.bitwise_and, grp="ci")
     ts(V("ci", 3, 4), V("ci", 0, 1), 2, A.logical_shift_right, 3, A.bitwise_and, grp="ci")
     ts(V("ci", 4, 5), V("ci", 0, 1), 1, A.logical_shift_right, 7, A.bitwise_and, grp="ci")
+    ts(V("ci", 5, 6), V("ci", 0, 1), 3, A.logical_shift_right, 1, A.bitwise_and, grp="ci")
     fill(V("wf"), 0.0)
-    cp(V("cl", GC, GC + 4), V("ci", 1, 5))
-    fill(V("wi", 512, 516), 0.0)
-    fill(V("wi", 3, 512, 4), 0.0)
+    cp(V("cl", GC, GC + 5), V("ci", 1, 6))
+    fill(V("wi"), 0.0)
     ts(V("c4", 4, 8), V("xm4", 0, 4), col(RC), A.is_equal, 1.0 / 128, A.mult)
     ts(col(C2), col(RH), 4.0, A.mult, 3.0, A.add)
     ts(V("df"), V("xm4"), col(QC), A.is_equal, 0.125, A.subtract)
-    scan(V("c4", 8, 12), V("c4", 0, 4), V("c4", 4, 8), A.mult, A.add)
-    ts(V("tl", 0, 21), V("n1"), 32.0, A.mult, col(C2), A.add)
-    fill(V("st", C, 512), 0.0)
-    ts(V("wr"), V("gc8"), col(GC), A.is_equal, V("c4", 11, 12), A.mult)
-    ts(V("tli", 0, 21), V("tl", 0, 21), 1.0 / 84, A.mult, -43.0 / 84, A.add)
     act(col(NR), col(RC), -1.0)
     act(col(HI), col(RC), -1.0, 15.0)
+    scan(V("c4", 8, 12), V("c4", 0, 4), V("c4", 4, 8), A.mult, A.add)
+    ts(V("tl", 0, 21), V("n1"), 32.0, A.mult, col(C2), A.add)
+    ts(V("hi"), V("dc"), col(HI), A.is_le, U, A.mult)
+    ts(V("wr"), V("gc8"), col(GC), A.is_equal, V("c4", 11, 12), A.mult)
+    ts(V("tli", 0, 21), V("tl", 0, 21), 1.0 / 84, A.mult, -43.0 / 84, A.add)
+    ts(V("lo"), V("dc"), col(NR), A.is_ge, U, A.mult)
+    fill(V("fs", 80, 84), 9.0)
     ts(V("wi", 2, 512, 4), V("dc"), 0.0, A.is_equal, -OWN * U, A.mult)
     ts(V("tl", 21, 42), V("tli", 0, 21), -84.0, A.mult)
-    ts(V("hi"), V("dc"), col(HI), A.is_le, U, A.mult)
-    ts(V("lo"), V("dc"), col(NR), A.is_ge, U, A.mult)
-    tt(V("tl", 42, 63), V("tl", 21, 42), V("tl", 0, 21), A.add)
-    fill(V("fs", 80, 84), 9.0)
-    cp(V("loh", 0, 21), V("tl", 42, 63))
     act(col(M0), col(QC), 0.125, -0.375)
     act(col(M1), col(QC), 0.125, -0.375 + 8.0 / 128)
     for t in range(4):
         acp(V("wf", 5 * t, 512, 16), V("wr"), grp="wf")
     act(V("mc", 0, 168), V("mc0"), 1.0 / 128, col(M0), grp="mc")
     act(V("mc", 168, 336), V("mc0"), 1.0 / 128, col(M1), grp="mc")
-    act(col(R21), col(RC), 21.0)
+    act(col(TM + 3), col(HB), -335.0)
     for v in (4, 3, 2, 1):
         s = 2.0 ** (v - 4)
-        act(col(N4 + 4 - v), col(QC), -16.0 * s, 48.5 * s + (1 << v) + 1023.5, grp="nb")
+        act(col(N4 + 4 - v), col(QC), -16.0 * s, 48.5 * s + (1 << v) + 1023.5 - (v == 3), grp="nb")
+    act(col(R21), col(RC), 42.0, col(TM + 3))
     sel(V("hi"), V("hi"), [[1, 128]], A.is_gt, 0.0, 0, -1)
     sel(V("wi", 1, 512, 4), V("lo"), [[-1, 128]], A.is_ge, 0.0, 0, 1)
     sel(V("wi", 0, 512, 4), V("hi"), [[1, 128]], A.not_equal, OWN * U, 0, -1)
-    for name, n in (("rst", 84), ("m2", 336), ("m16", 336)):
-        act(V(name), V("mc", 0, n), 0.0, 1.0)
-    act(V("thr"), V("mc", 0, 100), 0.0, OWN * U)
-    for name, n, st in (("rst", 84, 21), ("m2", 336, 2), ("m16", 336, 16)):
-        act(V(name, 0, n, st), V("mc", 0, n // st), 0.0)
-    act(V("thr", 0, 100, 5), V("mc", 0, 20), 0.0, 2.0)
-    act(V("tn", 0, 100, 5), V("n1", 0, 20), 0.0, (10240 + P0 - B0 - 10) / 10.0)
-    act(V("of2", 0, 100, 5), V("n1", 0, 20), 0.0, (-400 - OWN) * U)
-    act(V("of2", 1, 100, 5), V("n1", 0, 20), 0.0, (P0 - OWN + 10) * U)
+    sel(V("eb", 3, 515, 4), V("ones"), [[-1, 128]], A.is_equal, 0.0, 0, 1)
+
+    def const(name, a, b, st, c):
+        act(V(name, a, b, st), V("zer", 0, len(range(a, b, st))), 1.0, c)
+
+    for x in (("rst", 0, 84, 1, 1.0), ("r3", 3, 1011, 2, 0.0), ("cnt", 336, 344, 1, 0.0), ("rst", 0, 84, 21, 0.0),
+              ("r4", 0, 704, 4, -2.0), ("r4", 3, 704, 4, 10 * U), ("r3", 11, 1011, 12, -30 * U), ("r3", 13, 1011, 12, -2.0),
+              ("tn", 0, 100, 5, (10240 + P0 - B0 - 10) / 10.0)):
+        const(*x)
     quant("u", 0, 128, V("ut"))
     iota(V("hh"), [[0, TAB]], int(EMPTY))
     iota(V("jm"), [[1, 640]])
@@ -295,15 +294,26 @@ def rank_program(g, core, T, topo):
 
     def late_constants(stage):
         if stage == 0:
+            tt(V("tl", 42, 63), V("tl", 21, 42), V("tl", 0, 21), A.add)
             quant("f", 0, 128, V("wf"))
+            cp(V("loh", 0, 21), V("tl", 42, 63))
         if stage == 1:
             for e in (2, 1):
                 quant("i", 128 * e, 128 * e + 128, V("wi", e, 512 + e))
         if stage == 2:
             quant("i", 0, 128, V("wi", 0, 512))
         if stage == 3:
-            ts(V("ltr", 0, 21), V("n1"), col(R21), A.add)
+            ts(V("tl", 0, 11), V("n1", 0, 11), 2.0, A.mult, col(R21), A.add)
+            fill(V("m16"), 1.0)
+            cp(V("ltr", 0, 11), V("tl", 0, 11))
+            ts(V("ltr", 12, 23), V("tl", 0, 11), 21.0, A.add)
+            fill(V("m16", 0, 336, 16), 0.0)
+            for x in (("r2", 20, 2540, 6, 0.0), ("thr", 0, 100, 1, OWN * U), ("r2", 56, 2540, 60, -10 * U), ("r2", 62, 2540, 60, -2.0)):
+                const(*x)
         if stage == 4:
+            for x in (("thr", 0, 100, 5, 2.0), ("thr", 3, 100, 5, (OWN + 10) * U),
+                      ("of2", 0, 100, 5, (-400 - OWN) * U), ("of2", 1, 100, 5, (P0 - OWN + 10) * U)):
+                const(*x)
             act(col(R4), col(QC), -4.0, col(RC))
             act(col(R1), col(RH), -2.0, col(RC))
             act(col(TM), col(QC), -2560.0, 7680.0)
@@ -326,12 +336,8 @@ def rank_program(g, core, T, topo):
                 act(V("d8", 80 * x, 80 * x + 80), V("xm8"), 1.0, -512.0, grp="d8")
             act(plane(0, C, 416), V("sk"), 0.0)
             act(plane(1, C, 416), V("sk"), 0.0)
-        if stage == 9:
-            fill(V("eb"), 0.0)
-            fill(V("ones"), 1.0)
-            sel(V("eb", 3, 515, 4), V("ones"), [[-1, 128]], A.is_equal, 0.0, 0, 1)
-        if stage == 10:
-            for b in range(4):
+        if stage in (9, 10):
+            for b in (2 * stage - 18, 2 * stage - 17):
                 quant("e", 128 * b, 128 * b + 128, V("eb", 3 - b, 515 - b))
         if stage == 11:
             quant("v", 0, 128, V("vt"))
@@ -344,12 +350,12 @@ def rank_program(g, core, T, topo):
         first = t == 0
         G = lambda s: "%s%d" % (s, t)
         late = late_constants if first else (lambda stage: None)
-        for h in range(2):
-            quant("x", H * h, H * h + H, V("xx", 4 * H * h, 4 * H * h + 4 * H))
-            mx(h, "u", 0, "x", H * h, H * h + H)
+        for h, (a, b) in enumerate(runs):
+            quant("x", a, b, V("xx", 4 * a, 4 * b))
+            mx(h, "u", 0, "x", a, b)
         late(0)
-        for h in range(2):
-            ts(V("st", H * h, H * h + H), P(h, H), 0.0, A.is_ge, grp=G("st"))
+        for h, (a, b) in enumerate(runs):
+            ts(V("st", a, b), P(h, b - a), 0.0, A.is_ge, grp=G("st"))
         quant("s", 0, 128, V("st"))
         mx(2, "f", 0, "s", 0, 128)
         late(1)
@@ -369,22 +375,29 @@ def rank_program(g, core, T, topo):
         shift = (B0 - OWN + 10 - 10240) * U
         act(V("of1"), V("tn"), 10.0 * U, shift)
         for v in (2, 3, 4):
-            act(V("of2", v, 100, 5), V("tn", v - 1, 100, 5), 10.0 * U, shift, grp=G("of2"))
+            act(V("of2", v, 100, 5), V("tn", v - 1, 100, 5), 10.0 * U, shift + (0, -10, 10)[v - 2] * U, grp=G("of2"))
         late(3)
         for h in range(4):
             scan(V("cnt", 84 * h, 84 * h + 84), V("rst"), P(3 + h // 2, 168, h % 2, 2), A.mult, A.add, grp=G("cnt"))
-        ts(V("r4", 160, 336), I(V("cnt"), V("ltr", 10, 21)), 10 * U, A.max, 10 * U, A.subtract, grp=G("r4"))
-        act(V("r4", 0, 160), I(V("cnt"), V("ltr", 0, 10)), 1.0, -10 * U, F.Relu, grp=G("r4"))
+        ts(V("r4", 1, 704, 4), I(V("cnt"), V("ltr", 0, 11)), 10 * U, A.max, 10 * U, A.subtract, grp=G("r4"))
+        act(V("r4", 2, 704, 4), I(V("cnt"), V("ltr", 12, 23)), 1.0, -10 * U, F.Relu, grp=G("r4"))
+        act(V("gsm", 22, 23), V("r4", 641, 642), -1.0 / U, 10.0)
         late(4)
-        for v, at in ((4, 0), (3, 152), (2, 228)):
-            n = 21 << v
-            scan(V("tx", at, at + n), V("m2", 0, n), V("r%d" % v), A.mult, A.add)
-            scan(way(v), V("m16", 0, 320, 16 >> v), V("r%d" % v, 0, 20 << v), A.mult, A.max)
-            ts(V("r%d" % (v - 1)), V("tx", at + 1, at + n, 2), 10 * U, A.max, 10 * U, A.subtract)
-            late(9 - v)
-        act(V("gsm", 3, 10), V("tx", 309, 322, 2), -1.0 / U, 10.0, F.Relu)
-        tt(V("aq", E0, 1601 + E0, 80), V("r1", 0, 42, 2), V("r1", 1, 42, 2), A.add)
-        scan(way(1), V("m16", 0, 320, 8), V("r1", 0, 40), A.mult, A.max)
+        scan(V("r3", 0, 1008, 3), V("r4", 0, 672, 2), V("r4", 1, 672, 2), A.add, A.max)
+        tt(V("tx"), V("r4", 1, 640, 4), V("r4", 2, 640, 4), A.max)
+        late(5)
+        scan(V("r2", 0, 2520, 5), V("r3", 3, 1011, 2), V("zer", 0, 504), A.add, A.max)
+        scan(way(4, 8), V("m16", 0, 320, 2), V("tx"), A.mult, A.max)
+        scan(way(3, 8), V("m16", 0, 320, 2), V("r3", 3, 960, 6), A.mult, A.max)
+        late(6)
+        act(V("gsm", 9, 10), V("r4", 642, 643), -1.0 / U, V("gsm", 22, 23), F.Relu)
+        act(V("gsm", 5, 9), V("r2", 2415, 2520, 30), -1.0 / U, 30.0, F.Relu)
+        scan(V("r1"), V("r2", 20, 2540, 6), V("zer", 0, 420), A.add, A.max)
+        scan(way(2, 4), V("m16", 0, 320, 4), V("r2", 20, 2400, 30), A.mult, A.max)
+        late(7)
+        act(V("gsm", 3, 5), V("r1", 405, 420, 10), -1.0 / U, 10.0, F.Relu)
+        tt(V("aq", E0, 1601 + E0, 80), V("r1", 6, 420, 20), V("r1", 16, 420, 20), A.add)
+        scan(way(1, 2), V("m16", 0, 320, 8), V("r1", 6, 400, 10), A.mult, A.max)
         act(V("gsm", 1, 2), V("aq", 1600 + E0, 1601 + E0), -1.0 / U)
         acp(V("gr"), I(V("gsm"), V("lrep")))
         late(8)
@@ -392,22 +405,27 @@ def rank_program(g, core, T, topo):
         tt(V("vd"), own, V("thr"), A.is_lt)
         tt(V("cd", 0, 100), own, V("of1"), A.add)
         tt(V("cd", 100, 200), own, V("of2"), A.add)
-        scan(V("fin", 0, 100), V("vd"), V("cd", 0, 100), A.add, A.min, grp=G("fin"))
-        scan(V("fin", 100, 200), V("vd"), V("cd", 100, 200), A.add, A.min, grp=G("fin"))
-        ts(V("lp"), V("fin", 4, 200, 5), 1.0 / U, A.mult, 0.0, A.max)
+        scan(V("fin", 0, 100), V("vd"), V("cd", 0, 100), A.add, A.min)
+        scan(V("fin", 100, 200), V("vd"), V("cd", 100, 200), A.add, A.min)
+        ts(V("lp", 0, 20), V("fin", 4, 100, 5), 1.0 / U, A.mult)
+        ts(V("lp", 20, 40), V("fin", 104, 200, 5), 1.0 / U, A.mult, 0.0, A.max)
         scan(V("dd"), V("m16", 0, L), V("gr"), A.mult, A.add)
         scatter(V("hh"), V("lp", 0, 20), V("jm", 0, C))
         if t == R - 1:
             acp(V("obf"), I(V("tb"), V("lp", 0, 20)))
             store("y", T.ob[:], V("obf"), T.obf[0:128:16, :])
         tt(V("ns"), V("dd"), V("sk"), A.is_lt)
-        tt(V("gg"), I(V("hh"), V("lp", 20, 40)), V("jm", C, 2 * C), A.min)
+        for a, b in runs:
+            tt(V("gg", a, b), I(V("hh"), V("lp", 20 + a // 16, 20 + b // 16)), V("jm", C + a, C + b), A.min)
+        for a, b in runs:
+            scan(V("gs", a, b), V("dm", a, b), V("gg", a, b), A.add, A.min)
         scan(V("hw"), V("gr"), V("ns"), A.add, A.mult)
-        scan(V("gs"), V("dm"), V("gg"), A.add, A.min)
+        for a, b in runs:
+            ts(V("lm", a // 4, b // 4), V("gs", a + 3, b, 4), 4.0, A.mult, col(CZ), A.add)
         ts(V("lfix"), V("hw", 15, L, 16), -1.0, A.mult, V("dd", 9, 10), A.add)
-        ts(V("lm"), V("gs", 3, C, 4), 4.0, A.mult, col(CZ), A.add)
         win = V("xx", 4 * C, 12 * C)
-        acp(V("zm"), I(win, V("lm", CUT // 4, C // 4)))
+        acp(V("zm", 0, 256), I(win, V("lm", CUT // 4, CUT // 4 + 16)))
+        acp(V("zm", 256, 512), I(win, V("lm", CUT // 4 + 16, C // 4)))
         acp(V("ge"), I(V("hh"), V("lfix")))
         if t + 1 < R:
             iota(V("hh", B0 + 20, B0 + 160), [[0, 140]], int(EMPTY))
@@ -426,7 +444,7 @@ def rank_program(g, core, T, topo):
         for k in (1, 0, 3, 2):
             mx(k, "w", 128 * k, "z", CUT, C)
         if first:
-            quant("a0", L, 224, V("zer"))
+            quant("a0", L, 224, V("zer", 0, 512))
         for k in (0, 2):
             ts(plane(k, CUT, C), P(k, C - CUT), 0.015625, A.mult)
             acp(plane(k + 1, CUT, C), P(k + 1, C - CUT), 0.015625)
@@ -442,7 +460,7 @@ def rank_program(g, core, T, topo):
         late(9)
         scatter(V("inv"), V("le"), V("jv2"))
         if t + 1 < R:
-            quant("a%d" % (t + 1), L, 224, V("zer"))
+            quant("a%d" % (t + 1), L, 224, V("zer", 0, 512))
         scan(V("ivs"), V("d8"), V("inv", 0, C), A.add, A.min)
         late(10)
         ts(V("lsrc"), V("ivs", 7, C, 8), col(CE), A.add)
@@ -454,21 +472,22 @@ def rank_program(g, core, T, topo):
             mx(4 + k, "e", 128 * k, G("a"), 0, 128, pre=[(arr, 2 * n_in)] if k == 1 else [])
         for k in range(4):
             (cp if k % 2 == 0 else acp)(plane(k, C, 416), P(4 + k, L))
-        cp(V("xx", 0, 4 * C, 2), I(V("yd", 0, 832), V("lsrc")), grp=G("xx"))
-        acp(V("xx", 1, 4 * C, 2), I(V("yd", 832, 1664), V("lsrc")), grp=G("xx"))
+        for a, b in runs:
+            cp(V("xx", 4 * a, 4 * b, 2), I(V("yd", 0, 832), V("lsrc", a // 8, b // 8)), grp=G("xx%d" % a))
+            acp(V("xx", 4 * a + 1, 4 * b, 2), I(V("yd", 832, 1664), V("lsrc", a // 8, b // 8)), grp=G("xx%d" % a))
         if t + 1 < R:
             twins(t + 1)
 
-    for h in range(2):
-        quant("x", H * h, H * h + H, V("xx", 4 * H * h, 4 * H * h + 4 * H))
-        mx(h, "v", 0, "x", H * h, H * h + H)
-        store("y", T.oc[:, 4 * H * h:4 * H * h + 4 * H], V("qx", H * h, H * h + H), T.qx[:, H * h:H * h + H].bitcast(dt.uint8))
+    for h, (a, b) in enumerate(runs):
+        quant("x", a, b, V("xx", 4 * a, 4 * b))
+        mx(h, "v", 0, "x", a, b)
+        store("y", T.oc[:, 4 * a:4 * b], V("qx", a, b), T.qx[:, a:b].bitcast(dt.uint8))
     for k in range(4):
         store("ys"[k // 2], T.osc[4 * k:4 * k + 4, :], V("sx"), T.sx[32 * k:32 * k + 4, :])
         if k == 1:
-            acp(V("yo", 0, H), P(0, H))
-            store("s", T.y[:, 0:H], V("yo", 0, H))
-    cp(V("yo", H, C), P(1, H))
-    store("y", T.y[:, H:C], V("yo", H, C))
+            acp(V("yo", 0, CUT), P(0, CUT))
+            store("s", T.y[:, 0:CUT], V("yo", 0, CUT))
+    cp(V("yo", CUT, C), P(1, C - CUT))
+    store("y", T.y[:, CUT:C], V("yo", CUT, C))
     emit(ops, queues, T)
     g.wait_ge(T.sem.sent, 2 * R * n_out)

import numpy as np
from concourse.mybir import dt, AluOpType, ActivationFunctionType
from concourse.bass import DstId, RemoteDMATransfer

A = AluOpType
F = ActivationFunctionType
C, L, R = 320, 96, 3
TD = "float16"
U = 2.0 ** -11
OWN = 1024
P0, B0 = 2, 262
TAB = 592
EMPTY = 2048.0
CUT = 192
E0 = 28
PL = (0, 832, 416, 1248)
Q4, U8, BF, F32, I32, U16 = "float8_e4m3fn_x4", "uint8", "bfloat16", "float32", "int32", "uint16"

SCRATCH = {"ps": ("psum", [128, 4096], F32)}
for _d, _list in (
        (BF, "xx 3840 ut 512 vt 512 st 512 oh 1352 wf 512 wi 520 eb 520 zer 680 ones 128 dc 128 lo 128 hi 128 wr 32 zt 1280 zm 512 yd 1664 bt 512"),
        (Q4, "qw 512 qu 128 qv 128 qx 320 qz 320 qs 128 qo 338 qf 128 qi 384 qe 512 qb0 128 qb1 128 qb2 128 qa0 224 qa1 224 qa2 224"),
        (U8, "sw 512 su 128 sv 128 sx 320 sz 320 ss 128 so 338 sf 128 si 384 se 512 sb0 128 sb1 128 sb2 128 sa0 224 sa1 224 sa2 224"),
        (F32, "cl 32 c4 12 gc8 32 mc0 168 mc 336 xm4 80 xm8 80 df 80 n1 21 tl 64 rst 84 jm 640 jv2 192 sk0 96 sk 96 d8 320 "
              "tb 592 obf 320 fs 84 cnt 344 hh 592 gsm 24 gr 96 dd 96 ns 96 hw 96 ge 96 es 96 inv 736 ivs 320 yo 320"),
        (TD, "m16 336 dm 320 tx 160 r4 704 r3 1012 r2 2540 r1 420 aq 1712 tn 100 of1 100 of2 100 thr 100 vd 100 cd 200 fin 200 "
             "gg 320 gs 320"),
        (I32, "ci 8 tli 24"),
        (U16, "loh 22 ltr 24 lrep 6 lp 40 lm 80 lfix 6 le 12 lsrc 40")):
    _w = _list.split()
    for _k in range(0, len(_w), 2):
        SCRATCH[_w[_k]] = ("sbuf", [128, int(_w[_k + 1])], _d)
NS = 110
SEMAPHORES = ["s%d" % i for i in range(NS)] + ["arr0", "arr1", "arr2", "sent", "stored"]


def emit(ops, queues, T):
    known = {q: set() for q in queues}
    groups = {}
    for i, o in enumerate(ops):
        groups.setdefault(o["grp"] or i, []).append(i)

    def meet(xs, ys, only=None):
        return any(n == n2 and only in (None, n) and (m & m2).any() for (n, m) in xs for (n2, m2) in ys)

    seen, waits, needed = [], [], set()
    for i, o in enumerate(ops):
        mine = []
        for k in range(i - 1, -1, -1):
            e = ops[k]
            if k in known[o["q"]] or e["kind"] in ("remote", "store") or (o["acc"] and e["acc"] == o["acc"]):
                continue
            if meet(o["w"], e["w"] + e["r"]) or meet(o["r"], e["w"]) or (e["q"] != o["q"] and meet(o["r"], e["r"], "ps")):
                key = e["grp"] or k
                assert groups[key][-1] < i
                mine.append(key)
                needed.add(key)
                for j in groups[key]:
                    known[o["q"]].add(j)
                    known[o["q"]] |= seen[j]
        waits.append(mine)
        seen.append(set(known[o["q"]]))
    last = []
    tag = {}
    for i, o in enumerate(ops):
        key = o["grp"] or i
        if key not in needed or key in tag:
            continue
        step = 16 if o["kind"] == "dma" else 1
        cls = "dma" if o["kind"] == "dma" else "c"
        pick = None
        for s, (c, ks, n) in enumerate(last):
            if c == cls and all(k in seen[j] for k in ks for j in groups[key]):
                pick = s
                break
        if pick is None:
            last.append([cls, [], 0])
            pick = len(last) - 1
        last[pick][1] = groups[key]
        last[pick][2] += step * len(groups[key])
        tag[key] = (pick, last[pick][2], step)
    stores = 0
    for i, o in enumerate(ops):
        q = queues[o["q"]]
        key = o["grp"] or i
        for k in waits[i]:
            q.wait_ge(T.sem["s%d" % tag[k][0]], tag[k][1])
        for (s, n) in o["pre"]:
            q.wait_ge(s, n)
        ins = o["f"]()
        if o["kind"] == "store":
            ins.then_inc(T.sem.stored, 16)
            stores += 16
        elif key in tag:
            ins.then_inc(T.sem["s%d" % tag[key][0]], tag[key][2])
    queues["y"].wait_ge(T.sem.stored, stores)


def engine_mask(topo, src, dst):
    e = topo.engines(src, dst)
    m = 0
    for k in e:
        m |= 1 << k
    return m, len(e)


def rank_program(g, core, T, topo):
    rank = T.rank_of(core)
    if rank is None:
        return
    n_ranks = len(T.cores)
    nxt, prv = T.cores[(rank + 1) % n_ranks], T.cores[(rank - 1) % n_ranks]
    rid, pid = topo.addr(nxt, core)
    mask, n_out = engine_mask(topo, core, nxt)
    n_in = engine_mask(topo, prv, core)[1]
    queues = {"v": g.vector, "s": g.scalar, "t": g.tensor, "g": g, "y": g.sync}
    ops = []

    def V(name, a=0, b=None, step=1):
        w = SCRATCH[name][1][1]
        b = w if b is None else b
        m = np.zeros(w, bool)
        if name == "ps":
            m[a // 512 * 512:(b + 511) // 512 * 512] = True
        else:
            m[a:b:step] = True
        ap = T[name][:, a:b] if step == 1 else T[name][:, a:b:step]
        return (ap, [(name, m)])

    def I(win, off):
        return (win[0].indirect(off[0]), win[1] + off[1])

    def op(q, f, w, r, kind="c", pre=(), grp=None, acc=None):
        ww, rr = [], []
        for x in w:
            ww += x[1]
        for x in r:
            if isinstance(x, tuple):
                rr += x[1]
        ops.append({"q": q, "f": f, "w": ww, "r": rr, "kind": kind, "pre": list(pre), "grp": grp, "acc": acc})

    def a_(x):
        return x[0] if isinstance(x, tuple) else x

    def ts(out, x, s1, o0, s2=None, o1=None, grp=None):
        if o1 is None:
            op("v", lambda: g.vector.tensor_scalar(out[0], x[0], a_(s1), None, o0), [out], [x, s1], grp=grp)
        else:
            op("v", lambda: g.vector.tensor_scalar(out[0], x[0], a_(s1), a_(s2), o0, o1), [out], [x, s1, s2], grp=grp)

    def tt(out, x, y, o, grp=None):
        op("v", lambda: g.vector.tensor_tensor(out[0], x[0], y[0], o), [out], [x, y], grp=grp)

    def cp(out, x, grp=None):
        op("v", lambda: g.vector.tensor_copy(out[0], x[0]), [out], [x], grp=grp)

    def scatter(win, off, x):
        op("v", lambda: g.vector.tensor_copy(win[0].indirect(off[0]), x[0]), [win], [off, x])

    def scan(out, d0, d1, o0, o1, grp=None):
        op("v", lambda: g.vector.tensor_tensor_scan(out[0], d0[0], d1[0], 0.0, o0, o1), [out], [d0, d1], grp=grp)

    def fill(out, c, grp=None):
        op("v", lambda: g.vector.memset(out[0], c), [out], [], grp=grp)

    def quant(name, a, b, x):
        q, s = V("q" + name, a, b), V("s" + name, a, b)
        op("v", lambda: g.vector.quantize_mx(q[0], s[0], x[0]), [q, s], [x])

    def act(out, x, scale=1.0, bias=0.0, f=F.Identity, grp=None):
        op("s", lambda: g.scalar.activation(out[0], x[0], f, bias=a_(bias), scale=a_(scale)), [out], [x, scale, bias], grp=grp)

    def acp(out, x, scale=1.0, grp=None):
        op("s", lambda: g.scalar.activation(out[0], x[0], F.Copy, scale=a_(scale)), [out], [x, scale], grp=grp)

    def mx(bank, left, la, right, a, b, pre=(), start=True, stop=True, acc=None):
        out = V("ps", 512 * bank, 512 * bank + b - a)
        lq, ls, rq, rs = V("q" + left, la, la + 128), V("s" + left, la, la + 128), V("q" + right, a, b), V("s" + right, a, b)
        op("t", lambda: g.tensor.matmul_mx(out[0], lq[0], ls[0], rq[0], rs[0], start, stop), [out], [lq, ls, rq, rs], pre=pre,
           acc=acc, grp=acc)

    def iota(out, pat, base=0, cm=0, exact=False):
        if exact:
            op("g", lambda: g.iota(out[0], pat, base, cm), [out], [])
        else:
            op("g", lambda: g.iota(out[0], pat, base, cm, allow_small_or_imprecise_dtypes=True), [out], [])

    def sel(out, x, pat, cmp, fl, base, cm):
        op("g", lambda: g.affine_select(out[0], x[0], pat, cmp, fl, base, cm), [out], [x])

    def load(out, src, codes=False, q="y", grp=None):
        ap = out[0].bitcast(dt.uint8) if codes else out[0]
        op(q, lambda: queues[q].dma_start(ap, a_(src)), [out], [src], kind="dma", grp=grp)

    def store(q, dst, x, ap=None):
        op(q, lambda: queues[q].dma_start(dst, x[0] if ap is None else ap), [], [x], kind="store")

    def P(bank, n, a=0, step=1):
        return V("ps", 512 * bank + a, 512 * bank + n, step)

    def col(k):
        return V("cl", k, k + 1)

    def plane(k, a, b):
        return V("yd", PL[k] + a, PL[k] + b)

    def way(v, n):
        st = 80 // n
        return V("aq", 16 * v + E0 - 80 + st, 16 * v + E0 + 80 * 19 + 1, st)

    def twins(t):
        for k in (1, 2):
            load(V("xx", 4 * C * k, 4 * C * k + 4 * C), V("xx", 0, 4 * C), grp="tw%d" % t)

    GC, RC, QC, RH, HB, NR, C2, R21, M0, M1, N4, N3, N2, N1, R4, R1, CZ, CE, HI, TM = range(20)
    runs = ((0, CUT), (CUT, C))

    load(V("ut"), T.u[:], q="s")
    for a, b in runs:
        load(V("xx", 4 * a, 4 * b), T.x[:, 4 * a:4 * b])

    iota(V("ci", 0, 1), [[0, 1]], 0, 1, exact=True)
    fill(V("zer"), 0.0)
    for name, a, b in (("st", C, 512), ("oh", 0, 680), ("oh", 680, 1352), ("eb", 0, 520)):
        load(V(name, a, b), V("zer", 0, b - a), grp="z" + name)
    load(V("qw"), T.wc[:], codes=True)
    load(V("sw"), T.ws[:])
    load(V("vt"), T.v[:])
    twins(0)
    act(V("ones"), V("zer", 0, 128), 1.0, 1.0)
    fill(V("c4", 0, 4), 2.0)
    iota(V("xm4"), [[0, 20], [1, 4]])
    iota(V("gc8"), [[1, 8], [0, 4]])
    iota(V("n1"), [[1, 21]])
    iota(V("dc"), [[1, 128]], 0, -1)
    iota(V("mc0"), [[1, 4], [0, 21], [4, 2]])
    ts(V("ci", 1, 2), V("ci", 0, 1), 4, A.logical_shift_right, grp="ci")
    ts(V("ci", 2, 3), V("ci", 0, 1), 15, A.bitwise_and, grp="ci")
    ts(V("ci", 3, 4), V("ci", 0, 1), 2, A.logical_shift_right, 3, A.bitwise_and, grp="ci")
    ts(V("ci", 4, 5), V("ci", 0, 1), 1, A.logical_shift_right, 7, A.bitwise_and, grp="ci")
    ts(V("ci", 5, 6), V("ci", 0, 1), 3, A.logical_shift_right, 1, A.bitwise_and, grp="ci")
    fill(V("wf"), 0.0)
    cp(V("cl", GC, GC + 5), V("ci", 1, 6))
    fill(V("wi"), 0.0)
    ts(V("c4", 4, 8), V("xm4", 0, 4), col(RC), A.is_equal, 1.0 / 128, A.mult)
    ts(col(C2), col(RH), 4.0, A.mult, 3.0, A.add)
    ts(V("df"), V("xm4"), col(QC), A.is_equal, 0.125, A.subtract)
    act(col(NR), col(RC), -1.0)
    act(col(HI), col(RC), -1.0, 15.0)
    scan(V("c4", 8, 12), V("c4", 0, 4), V("c4", 4, 8), A.mult, A.add)
    ts(V("tl", 0, 21), V("n1"), 32.0, A.mult, col(C2), A.add)
    ts(V("hi"), V("dc"), col(HI), A.is_le, U, A.mult)
    ts(V("wr"), V("gc8"), col(GC), A.is_equal, V("c4", 11, 12), A.mult)
    ts(V("tli", 0, 21), V("tl", 0, 21), 1.0 / 84, A.mult, -43.0 / 84, A.add)
    ts(V("lo"), V("dc"), col(NR), A.is_ge, U, A.mult)
    fill(V("fs", 80, 84), 9.0)
    ts(V("wi", 2, 512, 4), V("dc"), 0.0, A.is_equal, -OWN * U, A.mult)
    ts(V("tl", 21, 42), V("tli", 0, 21), -84.0, A.mult)
    act(col(M0), col(QC), 0.125, -0.375)
    act(col(M1), col(QC), 0.125, -0.375 + 8.0 / 128)
    for t in range(4):
        acp(V("wf", 5 * t, 512, 16), V("wr"), grp="wf")
    act(V("mc", 0, 168), V("mc0"), 1.0 / 128, col(M0), grp="mc")
    act(V("mc", 168, 336), V("mc0"), 1.0 / 128, col(M1), grp="mc")
    act(col(TM + 3), col(HB), -335.0)
    for v in (4, 3, 2, 1):
        s = 2.0 ** (v - 4)
        act(col(N4 + 4 - v), col(QC), -16.0 * s, 48.5 * s + (1 << v) + 1023.5 - (v == 3), grp="nb")
    act(col(R21), col(RC), 42.0, col(TM + 3))
    sel(V("hi"), V("hi"), [[1, 128]], A.is_gt, 0.0, 0, -1)
    sel(V("wi", 1, 512, 4), V("lo"), [[-1, 128]], A.is_ge, 0.0, 0, 1)
    sel(V("wi", 0, 512, 4), V("hi"), [[1, 128]], A.not_equal, OWN * U, 0, -1)
    sel(V("eb", 3, 515, 4), V("ones"), [[-1, 128]], A.is_equal, 0.0, 0, 1)

    def const(name, a, b, st, c):
        act(V(name, a, b, st), V("zer", 0, len(range(a, b, st))), 1.0, c)

    for x in (("rst", 0, 84, 1, 1.0), ("r3", 3, 1011, 2, 0.0), ("cnt", 336, 344, 1, 0.0), ("rst", 0, 84, 21, 0.0),
              ("r4", 0, 704, 4, -2.0), ("r4", 3, 704, 4, 10 * U), ("r3", 11, 1011, 12, -30 * U), ("r3", 13, 1011, 12, -2.0),
              ("tn", 0, 100, 5, (10240 + P0 - B0 - 10) / 10.0)):
        const(*x)
    quant("u", 0, 128, V("ut"))
    iota(V("hh"), [[0, TAB]], int(EMPTY))
    iota(V("jm"), [[1, 640]])
    iota(V("xm8"), [[0, 10], [1, 8]])
    iota(V("sk0"), [[-16, 6], [10, 16]], B0)
    iota(V("sk0", 0, 96, 16), [[0, 6]], -9999)
    iota(V("sk0", 1, 96, 16), [[-16, 6]], P0)
    iota(V("gsm"), [[0, 24]])
    iota(V("gsm", 0, 4, 2), [[B0 + 8 - P0 - 10, 2]], P0 + 10)
    iota(V("jv2"), [[1, L], [0, 2]], C)
    iota(V("bt", 4 * L, 512), [[0, 128]])
    iota(V("inv", 0, C), [[1, C]])

    def late_constants(stage):
        if stage == 0:
            tt(V("tl", 42, 63), V("tl", 21, 42), V("tl", 0, 21), A.add)
            quant("f", 0, 128, V("wf"))
            cp(V("loh", 0, 21), V("tl", 42, 63))
        if stage == 1:
            for e in (2, 1):
                quant("i", 128 * e, 128 * e + 128, V("wi", e, 512 + e))
        if stage == 2:
            quant("i", 0, 128, V("wi", 0, 512))
        if stage == 3:
            ts(V("tl", 0, 11), V("n1", 0, 11), 2.0, A.mult, col(R21), A.add)
            fill(V("m16"), 1.0)
            cp(V("ltr", 0, 11), V("tl", 0, 11))
            ts(V("ltr", 12, 23), V("tl", 0, 11), 21.0, A.add)
            fill(V("m16", 0, 336, 16), 0.0)
            for x in (("r2", 20, 2540, 6, 0.0), ("thr", 0, 100, 1, OWN * U), ("r2", 56, 2540, 60, -10 * U), ("r2", 62, 2540, 60, -2.0)):
                const(*x)
        if stage == 4:
            for x in (("thr", 0, 100, 5, 2.0), ("thr", 3, 100, 5, (OWN + 10) * U),
                      ("of2", 0, 100, 5, (-400 - OWN) * U), ("of2", 1, 100, 5, (P0 - OWN + 10) * U)):
                const(*x)
            act(col(R4), col(QC), -4.0, col(RC))
            act(col(R1), col(RH), -2.0, col(RC))
            act(col(TM), col(QC), -2560.0, 7680.0)
            for x in range(4):
                act(V("dm", 80 * x, 80 * x + 80), V("df"), 3200.0, -240.0, grp="dm")
            act(V("gsm", 16, 22), V("n1", 0, 6), -16.0, col(NR))
            act(V("sk"), V("sk0"), 1.0, col(NR))
            act(col(CZ), col(TM), 1.0, col(R4))
            act(col(TM + 1), col(RH), -512.0, 3584.0)
            act(col(CE), col(R1), 416.0, col(TM + 1))
        if stage == 5:
            ts(V("tl", 0, 6), V("n1", 1, 7), 1.0, A.mult)
            ts(col(TM + 2), col(RC), 15.0, A.is_equal)
        if stage == 6:
            ts(V("lrep"), V("tl", 0, 6), col(TM + 2), A.mult, col(RC), A.add)
        if stage == 7:
            ts(V("xm8"), V("xm8"), col(RH), A.is_equal, 4608.0, A.mult)
        if stage == 8:
            for x in range(4):
                act(V("d8", 80 * x, 80 * x + 80), V("xm8"), 1.0, -512.0, grp="d8")
            act(plane(0, C, 416), V("sk"), 0.0)
            act(plane(1, C, 416), V("sk"), 0.0)
        if stage in (9, 10):
            for b in (2 * stage - 18, 2 * stage - 17):
                quant("e", 128 * b, 128 * b + 128, V("eb", 3 - b, 515 - b))
        if stage == 11:
            quant("v", 0, 128, V("vt"))
            iota(V("tb", B0, B0 + 320), [[1, 32], [0, 10]], -1)
            iota(V("tb", 0, B0 + 20), [[0, B0 + 20]], -1)
            iota(V("tb", P0, P0 + 10), [[0, 10]])
            iota(V("tb", B0 + 320, TAB), [[0, TAB - B0 - 320]])

    for t in range(R):
        first = t == 0
        G = lambda s: "%s%d" % (s, t)
        late = late_constants if first else (lambda stage: None)
        for h, (a, b) in enumerate(runs):
            quant("x", a, b, V("xx", 4 * a, 4 * b))
            mx(h, "u", 0, "x", a, b)
        late(0)
        for h, (a, b) in enumerate(runs):
            ts(V("st", a, b), P(h, b - a), 0.0, A.is_ge, grp=G("st"))
        quant("s", 0, 128, V("st"))
        mx(2, "f", 0, "s", 0, 128)
        late(1)
        scan(V("fs", 0, 80), V("df"), P(2, 80), A.add, A.min)
        late(2)
        tt(V("oh", 8, 776, 4), I(V("fs"), V("loh", 0, 12)), V("mc", 0, 192), A.is_equal)
        tt(V("oh", 776, 1352, 4), I(V("fs"), V("loh", 12, 21)), V("mc", 192, 336), A.is_equal)
        for v in (4, 3, 2, 1):
            act(V("tn", v, 100, 5), V("fs", 3, 80, 4), 128.0 * 2.0 ** (v - 4), col(N4 + 4 - v), grp=G("tn"))
        quant("o", 0, 170, V("oh", 0, 680))
        quant("o", 170, 338, V("oh", 680, 1352))
        for h in range(2):
            a = 168 * h
            mx(3 + h, "i", 0, "o", a + 2, a + 170, stop=False, acc=G("cn%d" % h))
            mx(3 + h, "i", 128, "o", a, a + 168, start=False, stop=False, acc=G("cn%d" % h))
            mx(3 + h, "i", 256, "o", a, a + 168, start=False, acc=G("cn%d" % h))
        shift = (B0 - OWN + 10 - 10240) * U
        act(V("of1"), V("tn"), 10.0 * U, shift)
        for v in (2, 3, 4):
            act(V("of2", v, 100, 5), V("tn", v - 1, 100, 5), 10.0 * U, shift + (0, -10, 10)[v - 2] * U, grp=G("of2"))
        late(3)
        for h in range(4):
            scan(V("cnt", 84 * h, 84 * h + 84), V("rst"), P(3 + h // 2, 168, h % 2, 2), A.mult, A.add, grp=G("cnt"))
        ts(V("r4", 1, 704, 4), I(V("cnt"), V("ltr", 0, 11)), 10 * U, A.max, 10 * U, A.subtract, grp=G("r4"))
        act(V("r4", 2, 704, 4), I(V("cnt"), V("ltr", 12, 23)), 1.0, -10 * U, F.Relu, grp=G("r4"))
        act(V("gsm", 22, 23), V("r4", 641, 642), -1.0 / U, 10.0)
        late(4)
        scan(V("r3", 0, 1008, 3), V("r4", 0, 672, 2), V("r4", 1, 672, 2), A.add, A.max)
        tt(V("tx"), V("r4", 1, 640, 4), V("r4", 2, 640, 4), A.max)
        late(5)
        scan(V("r2", 0, 2520, 5), V("r3", 3, 1011, 2), V("zer", 0, 504), A.add, A.max)
        scan(way(4, 8), V("m16", 0, 320, 2), V("tx"), A.mult, A.max)
        scan(way(3, 8), V("m16", 0, 320, 2), V("r3", 3, 960, 6), A.mult, A.max)
        late(6)
        act(V("gsm", 9, 10), V("r4", 642, 643), -1.0 / U, V("gsm", 22, 23), F.Relu)
        act(V("gsm", 5, 9), V("r2", 2415, 2520, 30), -1.0 / U, 30.0, F.Relu)
        scan(V("r1"), V("r2", 20, 2540, 6), V("zer", 0, 420), A.add, A.max)
        scan(way(2, 4), V("m16", 0, 320, 4), V("r2", 20, 2400, 30), A.mult, A.max)
        late(7)
        act(V("gsm", 3, 5), V("r1", 405, 420, 10), -1.0 / U, 10.0, F.Relu)
        tt(V("aq", E0, 1601 + E0, 80), V("r1", 6, 420, 20), V("r1", 16, 420, 20), A.add)
        scan(way(1, 2), V("m16", 0, 320, 8), V("r1", 6, 400, 10), A.mult, A.max)
        act(V("gsm", 1, 2), V("aq", 1600 + E0, 1601 + E0), -1.0 / U)
        acp(V("gr"), I(V("gsm"), V("lrep")))
        late(8)
        own = V("aq", E0, 1600 + E0, 16)
        tt(V("vd"), own, V("thr"), A.is_lt)
        tt(V("cd", 0, 100), own, V("of1"), A.add)
        tt(V("cd", 100, 200), own, V("of2"), A.add)
        scan(V("fin", 0, 100), V("vd"), V("cd", 0, 100), A.add, A.min)
        scan(V("fin", 100, 200), V("vd"), V("cd", 100, 200), A.add, A.min)
        ts(V("lp", 0, 20), V("fin", 4, 100, 5), 1.0 / U, A.mult)
        ts(V("lp", 20, 40), V("fin", 104, 200, 5), 1.0 / U, A.mult, 0.0, A.max)
        scan(V("dd"), V("m16", 0, L), V("gr"), A.mult, A.add)
        scatter(V("hh"), V("lp", 0, 20), V("jm", 0, C))
        if t == R - 1:
            acp(V("obf"), I(V("tb"), V("lp", 0, 20)))
            store("y", T.ob[:], V("obf"), T.obf[0:128:16, :])
        tt(V("ns"), V("dd"), V("sk"), A.is_lt)
        for a, b in runs:
            tt(V("gg", a, b), I(V("hh"), V("lp", 20 + a // 16, 20 + b // 16)), V("jm", C + a, C + b), A.min)
        for a, b in runs:
            scan(V("gs", a, b), V("dm", a, b), V("gg", a, b), A.add, A.min)
        scan(V("hw"), V("gr"), V("ns"), A.add, A.mult)
        for a, b in runs:
            ts(V("lm", a // 4, b // 4), V("gs", a + 3, b, 4), 4.0, A.mult, col(CZ), A.add)
        ts(V("lfix"), V("hw", 15, L, 16), -1.0, A.mult, V("dd", 9, 10), A.add)
        win = V("xx", 4 * C, 12 * C)
        acp(V("zm", 0, 256), I(win, V("lm", CUT // 4, CUT // 4 + 16)))
        acp(V("zm", 256, 512), I(win, V("lm", CUT // 4 + 16, C // 4)))
        acp(V("ge"), I(V("hh"), V("lfix")))
        if t + 1 < R:
            iota(V("hh", B0 + 20, B0 + 160), [[0, 140]], int(EMPTY))
        tt(V("zt", 0, 4 * CUT), I(win, V("lm", 0, CUT // 4)), V("xx", 0, 4 * CUT), A.add)
        tt(V("zt", 4 * CUT, 4 * CUT + 256), V("zm", 0, 256), V("xx", 4 * CUT, 4 * CUT + 256), A.add)
        quant("z", 0, CUT, V("zt", 0, 4 * CUT))
        tt(V("zt", 4 * CUT + 256, 4 * C), V("zm", 256, 512), V("xx", 4 * CUT + 256, 4 * C), A.add)
        for k in range(4):
            mx(4 + k, "w", 128 * k, "z", 0, CUT)
        for k in (0, 1, 3):
            acp(plane(k, 0, CUT), P(4 + k, CUT), 0.015625)
        scan(V("es"), V("d8", 0, L), V("ge"), A.add, A.min)
        quant("z", CUT, C, V("zt", 4 * CUT, 4 * C))
        ts(V("le"), V("es", 7, L, 8), col(CE), A.add)
        ts(plane(2, 0, CUT), P(6, CUT), 0.015625, A.mult)
        for k in (1, 0, 3, 2):
            mx(k, "w", 128 * k, "z", CUT, C)
        if first:
            quant("a0", L, 224, V("zer", 0, 512))
        for k in (0, 2):
            ts(plane(k, CUT, C), P(k, C - CUT), 0.015625, A.mult)
            acp(plane(k + 1, CUT, C), P(k + 1, C - CUT), 0.015625)
        cp(V("bt", 0, 4 * L, 2), I(V("yd", 0, 736), V("le")), grp=G("bt"))
        acp(V("bt", 1, 4 * L, 2), I(V("yd", 832, 1568), V("le")), grp=G("bt"))
        qb, sb, qa, sa = G("qb"), G("sb"), G("qa"), G("sa")
        quant(G("b"), 0, 128, V("bt"))
        arr = T.sem[G("arr")]
        op("g", lambda qa=qa, qb=qb, arr=arr: g.remote_dma(T[qa][:, 0:L].bitcast(dt.uint8), T[qb][:, 0:L].bitcast(dt.uint8),
                                                          arr, T.sem.sent, pid, rid, mask), [], [V(qb)], kind="remote")
        op("g", lambda sa=sa, sb=sb, arr=arr: g.remote_dma(T[sa][:, 0:L], T[sb][:, 0:L],
                                                          arr, T.sem.sent, pid, rid, mask), [], [V(sb)], kind="remote")
        late(9)
        scatter(V("inv"), V("le"), V("jv2"))
        if t + 1 < R:
            quant("a%d" % (t + 1), L, 224, V("zer", 0, 512))
        scan(V("ivs"), V("d8"), V("inv", 0, C), A.add, A.min)
        late(10)
        ts(V("lsrc"), V("ivs", 7, C, 8), col(CE), A.add)
        if t + 1 < R:
            iota(V("inv", 0, C), [[1, C]])
        if t == 1:
            late_constants(11)
        for k in (1, 0, 3, 2):
            mx(4 + k, "e", 128 * k, G("a"), 0, 128, pre=[(arr, 2 * n_in)] if k == 1 else [])
        for k in range(4):
            (cp if k % 2 == 0 else acp)(plane(k, C, 416), P(4 + k, L))
        for a, b in runs:
            cp(V("xx", 4 * a, 4 * b, 2), I(V("yd", 0, 832), V("lsrc", a // 8, b // 8)), grp=G("xx%d" % a))
            acp(V("xx", 4 * a + 1, 4 * b, 2), I(V("yd", 832, 1664), V("lsrc", a // 8, b // 8)), grp=G("xx%d" % a))
        if t + 1 < R:
            twins(t + 1)

    for h, (a, b) in enumerate(runs):
        quant("x", a, b, V("xx", 4 * a, 4 * b))
        mx(h, "v", 0, "x", a, b)
        store("y", T.oc[:, 4 * a:4 * b], V("qx", a, b), T.qx[:, a:b].bitcast(dt.uint8))
    for k in range(4):
        store("ys"[k // 2], T.osc[4 * k:4 * k + 4, :], V("sx"), T.sx[32 * k:32 * k + 4, :])
        if k == 1:
            acp(V("yo", 0, CUT), P(0, CUT))
            store("s", T.y[:, 0:CUT], V("yo", 0, CUT))
    cp(V("yo", CUT, C), P(1, C - CUT))
    store("y", T.y[:, CUT:C], V("yo", CUT, C))
    emit(ops, queues, T)
    g.wait_ge(T.sem.sent, 2 * R * n_out)
